import numpy as np
import ml_dtypes


def mxq(x, axis, fmt="e4m3"):
    dtype, down = {"e4m3": (ml_dtypes.float8_e4m3fn, 7), "e5m2": (ml_dtypes.float8_e5m2, 14)}[fmt]
    v = np.moveaxis(np.asarray(x, np.float32).astype(ml_dtypes.bfloat16).astype(np.float64), axis, -1)
    blocks = v.reshape(v.shape[:-1] + (-1, 32))
    amax = np.abs(blocks).max(-1, keepdims=True)
    byte = np.maximum(np.where(amax > 0, np.frexp(amax)[1] - 1 + 127, 0) - down, 1)
    scale = np.exp2(byte - 127.0)
    codes = (blocks / scale).astype(np.float32).astype(dtype).astype(np.float64)
    return np.moveaxis((codes * scale).reshape(v.shape), -1, axis)


WIDE = False


def mx_kscale(k):
    if not WIDE:
        return np.ones(k)
    levels = np.array([10, -10, 5, -5, 0])
    if k % 512:
        return np.exp2(np.random.permutation(np.resize(levels, k // 32))).repeat(32)
    a = np.empty((k // 512, 16))
    for p in range(k // 512):
        a[p, :8] = np.random.permutation(np.resize(levels, 8))
        for g in range(8):
            far = levels[np.abs(levels - a[p, g]) >= 10]
            a[p, g + 8] = far[np.random.randint(len(far))]
    return np.exp2(a.ravel()).repeat(32)


def f64(x):
    return np.asarray(x).astype(np.float64)


def striped(idx):
    return np.tile(idx.reshape(-1, 16).T, (8, 1)).astype(np.uint16)


def unstriped(offs):
    return offs[:16].T.reshape(-1).astype(np.int64)


E2M1 = np.array([0.0, 0.5, 1.0, 1.5, 2.0, 3.0, 4.0, 6.0, -0.0, -0.5, -1.0, -1.5, -2.0, -3.0, -4.0, -6.0])


def pack_weight(w, fmt):
    k, n = w.shape
    w = f64(np.asarray(w, np.float32).astype(ml_dtypes.bfloat16)).reshape(k // 32, 32, n)
    amax = np.abs(w).max(1)
    if fmt == "e4m3":
        byte = np.frexp(amax)[1] - 1 + 127 - 7
    else:
        mant, ex = np.frexp(amax / 6.0)
        byte = np.where(mant > 0.5, ex, ex - 1) + 127
    byte = np.clip(np.where(amax > 0, byte, 1), 1, 254)
    scaled = (w * np.exp2(127.0 - byte)[:, None, :]).reshape(k, n).astype(np.float32)
    by_word = np.ascontiguousarray(scaled.reshape(k // 512, 128, 4, n).transpose(0, 1, 3, 2))
    if fmt == "e4m3":
        words = by_word.astype(ml_dtypes.float8_e4m3fn).view(np.uint8)
    else:
        c = by_word.astype(ml_dtypes.float4_e2m1fn).view(np.uint8) & 0xF
        words = (c[..., 0::2] | (c[..., 1::2] << 4)).reshape(k // 512, 128, 2 * n)
    return np.ascontiguousarray(words), np.ascontiguousarray(byte.astype(np.uint8).reshape(k // 512, 16, n))


def unpack_weight(words, scales, fmt):
    g, _, n = scales.shape
    words = np.ascontiguousarray(words).reshape(g, 128, n, -1)
    if fmt == "e4m3":
        vals = words.view(ml_dtypes.float8_e4m3fn).astype(np.float64)
    else:
        nib = np.empty((g, 128, n, 4), np.uint8)
        nib[..., 0::2] = words & 0xF
        nib[..., 1::2] = words >> 4
        vals = E2M1[nib]
    vals = vals * np.repeat(np.exp2(scales.astype(np.float64) - 127.0), 8, axis=1)[..., None]
    return vals.transpose(0, 1, 3, 2).reshape(g * 512, n)


def gelu(v):
    return 0.5 * v * (1.0 + np.tanh(np.sqrt(2.0 / np.pi) * (v + 0.044715 * v**3)))


K, M, H, N, TA, TB, S, T2 = 1024, 512, 1024, 512, 2048, 1024, 512, 1024


def setup_inputs():
    n = np.random.standard_normal
    s, s2, u = mx_kscale(K)[:, None], mx_kscale(M)[:, None], mx_kscale(H)[:, None]
    tab_words, tab_scales = pack_weight(n((K, TA)) * s, "e4m3")
    tab2_words, tab2_scales = pack_weight(n((M, TB)) * s2, "e4m3")
    w2_words, w2_scales = pack_weight(n((M, H)) / np.sqrt(M) / s2 * u.T, "e4m3")
    wa_words, wa_scales = pack_weight(n((H, N)) / np.sqrt(H) / u, "e2m1")
    return {
        "tab_words": tab_words, "tab_scales": tab_scales,
        "tab2_words": tab2_words, "tab2_scales": tab2_scales,
        "offs": striped(np.random.permutation(TA)[:S]),
        "offs2": striped(np.random.permutation(TB)[:S]),
        "offs3": striped(np.random.permutation(T2)[:S]),
        "offs4": striped(np.random.permutation(T2)[:S]),
        "w1": (1.5 * n((K, H)) / np.sqrt(K) / s).astype(np.float32),
        "gain1": (1.2 * np.exp(0.3 * n(H)) * u[:, 0]).astype(np.float32),
        "w2_words": w2_words, "w2_scales": w2_scales,
        "wg1": np.exp(0.3 * n((128, S))).astype(np.float32),
        "wg2": np.exp(0.3 * n((128, S))).astype(np.float32),
        "refm": (0.8 * n((H, T2)) * u).astype(np.float32),
        "wa_words": wa_words, "wa_scales": wa_scales,
        "wb": (n((H, N)) / np.sqrt(H) / u).astype(np.float32),
    }


def reference(tab_words, tab_scales, tab2_words, tab2_scales, offs, offs2, offs3, offs4, w1, gain1,
              w2_words, w2_scales, wg1, wg2, refm, wa_words, wa_scales, wb):
    v = unpack_weight(tab_words, tab_scales, "e4m3")[:, unstriped(offs)]
    v2 = unpack_weight(tab2_words, tab2_scales, "e4m3")[:, unstriped(offs2)]
    h1 = np.tanh(mxq(f64(w1), 0, "e4m3").T @ v) * f64(gain1)[:, None]
    h2 = unpack_weight(w2_words, w2_scales, "e4m3").T @ v2
    pa = np.zeros((H, T2))
    pa[:, unstriped(offs3)] = np.tile(f64(wg1), (H // 128, 1)) * h1
    pb = np.zeros((H, T2))
    pb[:, unstriped(offs4)] = np.tile(f64(wg2), (H // 128, 1)) * h2
    z = np.sqrt(np.square(pa + f64(refm)) + np.square(pb))
    zq = mxq(z, 0, "e4m3")
    ya = unpack_weight(wa_words, wa_scales, "e2m1").T @ zq
    yb = mxq(f64(wb), 0, "e4m3").T @ zq
    return np.maximum(ya, yb)

@@ -1,0 +1,411 @@
+from contextlib import ExitStack
+
+import concourse.mybir as mybir
+from concourse.masks import make_identity
+
+F32 = mybir.dt.float32
+BF16 = mybir.dt.bfloat16
+I32 = mybir.dt.int32
+U32 = mybir.dt.uint32
+U16 = mybir.dt.uint16
+U8 = mybir.dt.uint8
+FP8X4 = mybir.dt.float8_e4m3fn_x4
+FP4X4 = mybir.dt.float4_e2m1fn_x4
+ACT = mybir.ActivationFunctionType
+ALU = mybir.AluOpType
+
+FLOPS = 3758096384
+
+P = 128
+S = 512
+T2 = 1024
+TA = 2048
+TB = 1024
+
+
+def tile_list_wavefront_mode_scores_kernel(
+    tc, tab_words, tab_scales, tab2_words, tab2_scales, offs, offs2, offs3, offs4, w1, gain1,
+    w2_words, w2_scales, wg1, wg2, refm, wa_words, wa_scales, wb, out,
+):
+    nc = tc.nc
+    with ExitStack() as ctx:
+        lists = ctx.enter_context(tc.tile_pool(name="lists", bufs=1))
+        keep = ctx.enter_context(tc.tile_pool(name="keep", bufs=1))
+        psum = ctx.enter_context(tc.psum_pool(name="psum", bufs=1))
+
+        def sb(name, shape, dtype, tag=None):
+            return keep.tile(shape, dtype, name=name, tag=tag or name, align_bytes=64)
+
+        list1 = lists.tile([P, S // 16], U16, name="list1")
+        list2 = lists.tile([P, S // 16], U16, name="list2")
+        list3 = lists.tile([P, S // 16], U16, name="list3")
+        list4 = lists.tile([P, S // 16], U16, name="list4")
+        bank = [psum.tile([P, 512], F32, name="bank%d" % i) for i in range(8)]
+
+        ident = sb("ident", [P, P], F32)
+        tabw = [sb("tabw%d" % g, [P, TA], U32, tag="big%d" % g) for g in range(2)]
+        tabs = sb("tabs", [P, TA], U8)
+        tab2w = sb("tab2w", [P, TB], U32)
+        tab2s = sb("tab2s", [P, TB], U8)
+        vw = [sb("vw%d" % g, [P, S], U32) for g in range(2)]
+        vs = sb("vs", [P, S], U8)
+        v2w = sb("v2w", [P, S], U32)
+        v2s = sb("v2s", [P, S], U8)
+        w2w = sb("w2w", [P, 1024], U32)
+        w2s = sb("w2s", [P, 1024], U8)
+        w2w_dealt = sb("w2w_dealt", [P, 512], U32)
+        w2s_dealt = sb("w2s_dealt", [P, 512], U8)
+        raw = [sb("raw%d" % i, [P, 2048], F32) for i in range(4)]
+        grouped = [sb("grouped%d" % i, [P, 2048], BF16) for i in range(4)]
+        w1c = [sb("w1c%d" % i, [P, 512], U32) for i in range(4)]
+        w1s = [sb("w1s%d" % i, [P, 512], U8) for i in range(4)]
+        wbc = [sb("wbc%d" % i, [P, 512], U32) for i in range(2)]
+        wbs = [sb("wbs%d" % i, [P, 512], U8) for i in range(2)]
+        waw = sb("waw", [P, 2048], U8)
+        was = sb("was", [P, 1024], U8)
+        wg1n = sb("wg1n", [P, S], F32)
+        wg2n = sb("wg2n", [P, S], F32)
+        gain = [sb("gain%d" % a, [P, 4], F32) for a in range(2)]
+        slope4 = [sb("slope4_%d" % a, [P, 4 * S], F32) for a in range(2)]
+        wind4 = [sb("wind4_%d" % a, [P, 4 * S], F32) for a in range(2)]
+        th = [slope4[s // 4][:, S * (s % 4) : S * (s % 4 + 1)] for s in range(8)]
+        hw = [wind4[s // 4][:, S * (s % 4) : S * (s % 4 + 1)] for s in range(8)]
+        ref = [sb("ref%d" % i, [P, T2], F32) for i in range(4)]
+        page_a = [sb("page_a%d" % i, [P, T2], F32) for i in range(4)]
+        page_b = [sb("page_b%d" % i, [P, T2], F32) for i in range(4)]
+        qt_second = sb("qt_second", [P, 2048], F32)
+        qt_flat = (raw[0], qt_second)
+        qt = [half[:].rearrange("p (c t r) -> p c t r", c=4, t=4) for half in qt_flat]
+        zb = sb("zb", [P, 4 * T2], BF16)
+        zc = [sb("zc%d" % a, [P, T2], U32) for a in range(2)]
+        zs = [sb("zs%d" % a, [P, T2], U8) for a in range(2)]
+
+        for plane in (tab2s, w2s, was):
+            nc.vector.memset(plane[:].bitcast(I32), 0)
+        for page in page_b:
+            nc.vector.memset(page[:], 0.0)
+
+        def load_words(dst, words):
+            nc.sync.dma_start(out=dst[:].bitcast(I32), in_=words.rearrange("p t i -> p (t i)").bitcast(I32))
+
+        def load_rows(dst, weight, g, a):
+            rows = weight[512 * g : 512 * (g + 1), 512 * a : 512 * (a + 1)]
+            nc.sync.dma_start(
+                out=dst[:].rearrange("p (j c) -> p j c", j=4), in_=rows.rearrange("(p j) c -> p j c", j=4)
+            )
+
+        def load_ref(s):
+            if s < 4:
+                rows = refm[P * s : P * (s + 1), :]
+            else:
+                rows = refm[512:1024, :].rearrange("(p t) j -> t p j", t=4)[s - 4]
+            nc.sync.dma_start(out=ref[s % 4][:], in_=rows)
+
+        def load_dealt(dst, wg):
+            for q in range(4):
+                nc.gpsimd.dma_start(out=dst[32 * q : 32 * (q + 1), :], in_=wg.rearrange("(p t) j -> p (t j)", t=4))
+
+        nc.sync.dma_start(list2[:], offs2)
+        load_words(tab2w, tab2_words[0])
+        for q in range(4):
+            nc.sync.dma_start(
+                out=tab2s[32 * q : 32 * q + 4, :].bitcast(I32), in_=tab2_scales[0, 4 * q : 4 * q + 4, :].bitcast(I32)
+            )
+        load_words(w2w, w2_words[0])
+        for q in range(4):
+            nc.sync.dma_start(
+                out=w2s[32 * q : 32 * q + 4, :].bitcast(I32), in_=w2_scales[0, 4 * q : 4 * q + 4, :].bitcast(I32)
+            )
+        nc.sync.dma_start(list1[:], offs)
+        nc.sync.dma_start(out=wg2n[:], in_=wg2)
+        nc.sync.dma_start(list4[:], offs4)
+        load_rows(raw[0], w1, 0, 0)
+        load_words(tabw[0], tab_words[0])
+        load_words(tabw[1], tab_words[1])
+        load_rows(raw[1], w1, 1, 0)
+        nc.sync.dma_start(list3[:], offs3)
+        nc.sync.dma_start(out=wg1n[:], in_=wg1)
+        load_rows(raw[2], w1, 0, 1)
+        load_rows(raw[3], w1, 1, 1)
+        for s in range(4):
+            load_ref(s)
+
+        nc.gpsimd.memset(tabs[:].bitcast(I32), 0)
+        for q in range(4):
+            nc.gpsimd.dma_start(
+                out=tabs[32 * q : 32 * q + 8, :].bitcast(I32), in_=tab_scales[:, 4 * q : 4 * q + 4, :].bitcast(I32)
+            )
+        make_identity(nc, ident[:])
+        for page in page_a:
+            nc.gpsimd.memset(page[:], 0.0)
+        with nc.allow_non_contiguous_dma(reason="one gain a partition"):
+            nc.gpsimd.dma_start(out=gain[0][:], in_=gain1[0:512].rearrange("(b p) -> p b", p=P))
+        nc.gpsimd.dma_start(out=gain[1][:], in_=gain1[512:1024].rearrange("(p t) -> p t", t=4))
+        for q in range(4):
+            nc.gpsimd.dma_start(
+                out=was[32 * q : 32 * q + 4, :].bitcast(I32).rearrange("p (a n) -> p a n", a=2),
+                in_=wa_scales[:, 4 * q : 4 * q + 4, :].bitcast(I32).rearrange("a r n -> r a n"),
+            )
+        nc.gpsimd.dma_start(
+            out=waw[:].bitcast(I32).rearrange("p (a c) -> p a c", a=2),
+            in_=wa_words.bitcast(I32).rearrange("a p c -> p a c"),
+        )
+
+        def cast(i, rows, dealt):
+            if dealt:
+                dst = grouped[i][:].rearrange("p (t m j) -> p m t j", t=4, j=4)
+                src = rows[:].rearrange("p (j m t) -> p m t j", j=4, t=4)
+            else:
+                dst = grouped[i][:].rearrange("p (c i j) -> p c j i", i=4, j=4)
+                src = rows[:].rearrange("p (j c i) -> p c j i", j=4, i=4)
+            nc.scalar.copy(out=dst, in_=src)
+
+        def quantize(codes, scales, values):
+            nc.vector.quantize_mx(out=codes.bitcast(FP8X4), scales=scales, in_=values)
+
+        def wind_features(s, b):
+            cols = slice(P * (s % 4), P * (s % 4 + 1))
+            words, scales = (w2w, w2s) if s < 4 else (w2w_dealt, w2s_dealt)
+            nc.tensor.matmul_mx(
+                out=bank[b][:], lhsT=words[:, cols].bitcast(FP8X4), lhsT_scale=scales[:, cols],
+                rhs=v2w[:].bitcast(FP8X4), rhs_scale=v2s[:], start=True, stop=True,
+            )
+            nc.scalar.copy(out=wind_source(s), in_=bank[b][:])
+
+        def slope_tanh(s, b):
+            cols = slice(P * (s % 4), P * (s % 4 + 1))
+            for g in range(2):
+                i = 2 * (s // 4) + g
+                nc.tensor.matmul_mx(
+                    out=bank[b][:], lhsT=w1c[i][:, cols].bitcast(FP8X4), lhsT_scale=w1s[i][:, cols],
+                    rhs=vw[g][:].bitcast(FP8X4), rhs_scale=vs[4 * g : P, :], start=(g == 0), stop=(g == 1),
+                )
+            nc.scalar.activation(out=th[s], in_=bank[b][:], func=ACT.Tanh)
+
+        def slope_source(s):
+            return th[s] if s < 6 else turned(s - 2, 1)
+
+        def wind_source(s):
+            return raw[1][:, 0:S] if s == 3 else turned(6, 1) if s == 7 else hw[s]
+
+        def slope_gain(s):
+            nc.scalar.activation(
+                out=slope_source(s), in_=th[s], func=ACT.Copy, scale=gain[s // 4][:, s % 4 : s % 4 + 1]
+            )
+
+        def slope_page(s):
+            return page_a[s if s < 4 else s % 2]
+
+        def scatter_a(s):
+            wg = wg1n[:] if s < 4 else th[s % 4]
+            nc.vector.tensor_tensor(slope_page(s)[:].indirect(list3[:]), slope_source(s), wg, ALU.mult)
+
+        def wind_page(s):
+            return page_b[(s + s // 4 * 3) % 4]
+
+        def scatter_b(s):
+            wg = wg2n[:] if s < 4 else raw[1][:, S * (s % 4) : S * (s % 4 + 1)]
+            nc.vector.tensor_tensor(wind_page(s)[:].indirect(list4[:]), wind_source(s), wg, ALU.mult)
+
+        def turn(dst, src, start, stop):
+            nc.tensor.matmul(dst, src, ident[:], start=start, stop=stop, is_transpose=True)
+
+        def turned(s, h):
+            return st_flat[h][:, S * (s % 4) : S * (s % 4 + 1)]
+
+        def back_bank(s, h):
+            return bank[(2, 6, 2, 4)[s % 4] + h]
+
+        def turn_square(s, terms, b0, dst):
+            for h in range(2):
+                b = bank[b0 + h]
+                for n, term in enumerate(terms):
+                    for c in range(4):
+                        j0 = 512 * h + P * c
+                        turn(b[:, P * c : P * (c + 1)], term[:, j0 : j0 + P],
+                             n == 0 and c == 0, n == len(terms) - 1 and c == 3)
+                if s < 4:
+                    nc.scalar.activation(
+                        out=dst[h][:, :, :, 32 * s : 32 * (s + 1)],
+                        in_=b[:].rearrange("p (c q t) -> p c t q", c=4, t=4), func=ACT.Square,
+                    )
+                else:
+                    nc.scalar.activation(
+                        out=turned(s, h), in_=b[:], func=ACT.Square
+                    )
+
+        def magnitude_turned(jc):
+            b = bank[2 + jc % 4]
+            for n, term in enumerate((qt, st)):
+                for t in range(4):
+                    turn(b[:, P * t : P * (t + 1)], term[jc // 4][:, jc % 4, t, :],
+                         n == 0 and t == 0, n == 1 and t == 3)
+            nc.scalar.activation(
+                out=zb[:, 512 * jc : 512 * (jc + 1)].rearrange("p (j t) -> p j t", t=4),
+                in_=b[:].rearrange("p (t j) -> p j t", t=4), func=ACT.Sqrt,
+            )
+
+        def zsq(s):
+            t = s % 4
+            return qt_flat[t // 2][:, T2 * (t % 2) : T2 * (t % 2 + 1)]
+
+        def square_b(s):
+            nc.scalar.activation(out=zsq(s), in_=wind_page(s)[:], func=ACT.Square)
+
+        def turn_back(s):
+            for h in range(2):
+                for c in range(4):
+                    turn(back_bank(s, h)[:, P * c : P * (c + 1)], turned(s, h)[:, P * c : P * (c + 1)], True, True)
+
+        def add_squares(s, j0, j1):
+            h = j0 // 512
+            nc.vector.tensor_tensor(
+                zsq(s)[:, j0:j1], back_bank(s, h)[:, j0 - 512 * h : j1 - 512 * h], zsq(s)[:, j0:j1], ALU.add
+            )
+
+        def root_pair(u, j0, j1):
+            nc.scalar.activation(
+                out=zb[:].rearrange("p (j t) -> p j t", t=4)[:, j0:j1, 2 * u : 2 * u + 2],
+                in_=qt_flat[u][:].rearrange("p (t j) -> p j t", t=2)[:, j0:j1, :], func=ACT.Sqrt,
+            )
+
+        def quantize_z(a, j0, j1):
+            quantize(zc[a][:, j0:j1], zs[a][:, j0:j1], zb[:, 4 * j0 : 4 * j1])
+
+        pair_banks = (6, 2, 0, 4)
+
+        def score_pass(i, a, j0, j1, start, stop, which=(0, 1)):
+            h = j0 // 512
+            cols = slice(P * i, P * (i + 1))
+            stationary = (
+                (waw[:, 1024 * a + 256 * i : 1024 * a + 256 * (i + 1)].bitcast(FP4X4),
+                 was[:, 512 * a + P * i : 512 * a + P * (i + 1)]),
+                (wbc[a][:, cols].bitcast(FP8X4), wbs[a][:, cols]),
+            )
+            for n in which:
+                codes, scales = stationary[n]
+                nc.tensor.matmul_mx(
+                    out=bank[pair_banks[i] + n][:, j0 - 512 * h : j1 - 512 * h], lhsT=codes, lhsT_scale=scales,
+                    rhs=zc[a][:, j0:j1].bitcast(FP8X4), rhs_scale=zs[a][:, j0:j1], start=start, stop=stop,
+                )
+
+        def larger_score(i, h):
+            first, result = th[i], th[4 + i]
+            nc.scalar.copy(out=first, in_=bank[pair_banks[i]][:])
+            nc.vector.tensor_tensor(result, bank[pair_banks[i] + 1][:], first, ALU.max)
+            nc.sync.dma_start(out=out[P * i : P * (i + 1), 512 * h : 512 * (h + 1)], in_=result)
+
+        def slope_square(s):
+            turn_square(s, (ref[s % 4], slope_page(s)), 0, st)
+            if s < 4:
+                load_ref(s + 4)
+
+        def wind_square(s):
+            turn_square(s, (page_b[s],), 0, qt)
+
+        nc.vector.tensor_copy(v2w[:], tab2w[:].indirect(list2[:]))
+        nc.vector.tensor_copy(v2s[:], tab2s[:].indirect(list2[:]))
+        nc.vector.tensor_copy(
+            w2w_dealt[:].bitcast(I32).rearrange("p (t m) -> p t m", t=4),
+            w2w[:, 512:1024].bitcast(I32).rearrange("p (m t) -> p t m", t=4),
+        )
+        nc.vector.tensor_copy(
+            w2s_dealt[:].rearrange("p (t m) -> p t m", t=4), w2s[:, 512:1024].rearrange("p (m t) -> p t m", t=4)
+        )
+        nc.vector.tensor_copy(vs[:], tabs[:].indirect(list1[:]))
+        for s in range(3):
+            wind_features(s, 4 + s)
+            scatter_b(s)
+        for s in range(4, 7):
+            wind_features(s, s - 2)
+        for g in range(2):
+            nc.vector.tensor_copy(vw[g][:], tabw[g][:].indirect(list1[:]))
+        for i in range(2):
+            cast(i, raw[i], False)
+            quantize(w1c[i][:], w1s[i][:], grouped[i][:])
+        wind_square(0)
+        wind_square(1)
+        wind_features(3, 1)
+        scatter_b(3)
+        load_dealt(raw[1], wg2)
+        st_flat = [sb("st%d" % h, [P, 4 * S], F32, tag="big%d" % h) for h in range(2)]
+        st = [half[:].rearrange("p (c t r) -> p c t r", c=4, t=4) for half in st_flat]
+        slope_tanh(0, 0)
+        slope_gain(0)
+        slope_tanh(1, 5)
+        slope_gain(1)
+        scatter_a(0)
+        wind_square(2)
+        for i in (2, 3):
+            cast(i, raw[i], True)
+            quantize(w1c[i][:], w1s[i][:], grouped[i][:])
+            load_rows(raw[i], wb, i - 2, 0)
+        scatter_a(1)
+        slope_tanh(2, 6)
+        slope_gain(2)
+        slope_tanh(3, 7)
+        slope_gain(3)
+        scatter_a(2)
+        scatter_a(3)
+        load_dealt(slope4[0], wg1)
+        slope_square(0)
+        wind_square(3)
+        slope_square(1)
+        for s in range(4, 8):
+            slope_tanh(s, s)
+        slope_gain(4)
+        slope_gain(5)
+        scatter_b(4)
+        slope_square(2)
+        slope_square(3)
+        scatter_b(5)
+        scatter_b(6)
+        for jc in range(8):
+            magnitude_turned(jc)
+        scatter_a(4)
+        quantize_z(0, 0, T2)
+        scatter_a(5)
+        for s in range(4, 7):
+            if s < 6:
+                cast(s - 4, raw[s - 2], False)
+                quantize(wbc[s - 4][:], wbs[s - 4][:], grouped[s - 4][:])
+            square_b(s)
+            slope_square(s)
+            turn_back(s)
+            for h in range(2):
+                add_squares(s, 512 * h, 512 * (h + 1))
+            if s < 6:
+                slope_gain(s + 2)
+                scatter_a(s + 2)
+        wind_features(7, 4)
+        scatter_b(7)
+        for h in range(2):
+            root_pair(0, 512 * h, 512 * (h + 1))
+        score_pass(0, 0, 0, 512, True, False)
+        slope_square(7)
+        turn_back(7)
+        score_pass(1, 0, 0, 512, True, False)
+        score_pass(2, 0, 0, 512, True, False)
+        last_page = wind_page(7)
+        for h in range(2):
+            for j0 in (512 * h, 512 * h + 256):
+                nc.vector.tensor_tensor(
+                    zsq(7)[:, j0 : j0 + 256], last_page[:, j0 : j0 + 256], last_page[:, j0 : j0 + 256], ALU.mult
+                )
+            for j0 in (512 * h, 512 * h + 256):
+                add_squares(7, j0, j0 + 256)
+                root_pair(1, j0, j0 + 256)
+            if h == 1:
+                score_pass(3, 0, 0, 512, True, False)
+            for j0 in (512 * h, 512 * h + 256):
+                quantize_z(1, j0, j0 + 256)
+        for j0 in (0, 256):
+            for i in range(4):
+                score_pass(i, 1, j0, j0 + 256, False, j0 == 256)
+        for i in range(4):
+            larger_score(i, 0)
+            for n in range(2):
+                score_pass(i, 0, 512, 1024, True, False, (n,))
+                score_pass(i, 1, 512, 1024, False, True, (n,))
+        for i in range(4):
+            larger_score(i, 1)

@@ -82,8 +82,10 @@ def tile_list_wavefront_mode_scores_kernel(
 
         for plane in (tab2s, w2s, was):
             nc.vector.memset(plane[:].bitcast(I32), 0)
-        for page in page_b:
+        for page in page_b[:2]:
             nc.vector.memset(page[:], 0.0)
+
+        nc.gpsimd.memset(tabs[:].bitcast(I32), 0)
 
         def load_words(dst, words):
             nc.sync.dma_start(out=dst[:].bitcast(I32), in_=words.rearrange("p t i -> p (t i)").bitcast(I32))
@@ -116,6 +118,10 @@ def tile_list_wavefront_mode_scores_kernel(
             nc.sync.dma_start(
                 out=w2s[32 * q : 32 * q + 4, :].bitcast(I32), in_=w2_scales[0, 4 * q : 4 * q + 4, :].bitcast(I32)
             )
+        for q in range(4):
+            (nc.gpsimd if q < 2 else nc.sync).dma_start(
+                out=tabs[32 * q : 32 * q + 8, :].bitcast(I32), in_=tab_scales[:, 4 * q : 4 * q + 4, :].bitcast(I32)
+            )
         nc.sync.dma_start(list1[:], offs)
         nc.sync.dma_start(out=wg2n[:], in_=wg2)
         nc.sync.dma_start(list4[:], offs4)
@@ -124,39 +130,36 @@ def tile_list_wavefront_mode_scores_kernel(
         load_words(tabw[1], tab_words[1])
         load_rows(raw[1], w1, 1, 0)
         nc.sync.dma_start(list3[:], offs3)
+        with nc.allow_non_contiguous_dma(reason="one gain a partition"):
+            nc.sync.dma_start(out=gain[0][:], in_=gain1[0:512].rearrange("(b p) -> p b", p=P))
+        nc.sync.dma_start(out=gain[1][:], in_=gain1[512:1024].rearrange("(p t) -> p t", t=4))
         nc.sync.dma_start(out=wg1n[:], in_=wg1)
+        load_ref(0)
         load_rows(raw[2], w1, 0, 1)
         load_rows(raw[3], w1, 1, 1)
-        for s in range(4):
+        for s in range(1, 4):
             load_ref(s)
-
-        nc.gpsimd.memset(tabs[:].bitcast(I32), 0)
         for q in range(4):
-            nc.gpsimd.dma_start(
-                out=tabs[32 * q : 32 * q + 8, :].bitcast(I32), in_=tab_scales[:, 4 * q : 4 * q + 4, :].bitcast(I32)
-            )
-        make_identity(nc, ident[:])
-        for page in page_a:
-            nc.gpsimd.memset(page[:], 0.0)
-        with nc.allow_non_contiguous_dma(reason="one gain a partition"):
-            nc.gpsimd.dma_start(out=gain[0][:], in_=gain1[0:512].rearrange("(b p) -> p b", p=P))
-        nc.gpsimd.dma_start(out=gain[1][:], in_=gain1[512:1024].rearrange("(p t) -> p t", t=4))
-        for q in range(4):
-            nc.gpsimd.dma_start(
+            nc.sync.dma_start(
                 out=was[32 * q : 32 * q + 4, :].bitcast(I32).rearrange("p (a n) -> p a n", a=2),
                 in_=wa_scales[:, 4 * q : 4 * q + 4, :].bitcast(I32).rearrange("a r n -> r a n"),
             )
-        nc.gpsimd.dma_start(
+        nc.sync.dma_start(
             out=waw[:].bitcast(I32).rearrange("p (a c) -> p a c", a=2),
             in_=wa_words.bitcast(I32).rearrange("a p c -> p a c"),
         )
 
-        def cast(i, rows, dealt):
+
+        make_identity(nc, ident[:])
+        for page in page_b[2:] + page_a:
+            nc.gpsimd.memset(page[:], 0.0)
+
+        def cast(values, rows, dealt):
             if dealt:
-                dst = grouped[i][:].rearrange("p (t m j) -> p m t j", t=4, j=4)
+                dst = values.rearrange("p (t m j) -> p m t j", t=4, j=4)
                 src = rows[:].rearrange("p (j m t) -> p m t j", j=4, t=4)
             else:
-                dst = grouped[i][:].rearrange("p (c i j) -> p c j i", i=4, j=4)
+                dst = values.rearrange("p (c i j) -> p c j i", i=4, j=4)
                 src = rows[:].rearrange("p (j c i) -> p c j i", j=4, i=4)
             nc.scalar.copy(out=dst, in_=src)
 
@@ -174,11 +177,11 @@ def tile_list_wavefront_mode_scores_kernel(
 
         def slope_tanh(s, b):
             cols = slice(P * (s % 4), P * (s % 4 + 1))
-            for g in range(2):
+            for g in (1, 0):
                 i = 2 * (s // 4) + g
                 nc.tensor.matmul_mx(
                     out=bank[b][:], lhsT=w1c[i][:, cols].bitcast(FP8X4), lhsT_scale=w1s[i][:, cols],
-                    rhs=vw[g][:].bitcast(FP8X4), rhs_scale=vs[4 * g : P, :], start=(g == 0), stop=(g == 1),
+                    rhs=vw[g][:].bitcast(FP8X4), rhs_scale=vs[4 * g : P, :], start=(g == 1), stop=(g == 0),
                 )
             nc.scalar.activation(out=th[s], in_=bank[b][:], func=ACT.Tanh)
 
@@ -211,7 +214,7 @@ def tile_list_wavefront_mode_scores_kernel(
             nc.tensor.matmul(dst, src, ident[:], start=start, stop=stop, is_transpose=True)
 
         def turned(s, h):
-            return st_flat[h][:, S * (s % 4) : S * (s % 4 + 1)]
+            return qt_flat[h][:, S * (s % 4) : S * (s % 4 + 1)]
 
         def back_bank(s, h):
             return bank[(2, 6, 2, 4)[s % 4] + h]
@@ -235,7 +238,7 @@ def tile_list_wavefront_mode_scores_kernel(
                     )
 
         def magnitude_turned(jc):
-            b = bank[2 + jc % 4]
+            b = bank[(2 + jc) % 8]
             for n, term in enumerate((qt, st)):
                 for t in range(4):
                     turn(b[:, P * t : P * (t + 1)], term[jc // 4][:, jc % 4, t, :],
@@ -247,7 +250,7 @@ def tile_list_wavefront_mode_scores_kernel(
 
         def zsq(s):
             t = s % 4
-            return qt_flat[t // 2][:, T2 * (t % 2) : T2 * (t % 2 + 1)]
+            return (st_flat[1], raw[2])[t // 2][:, T2 * (t % 2) : T2 * (t % 2 + 1)]
 
         def square_b(s):
             nc.scalar.activation(out=zsq(s), in_=wind_page(s)[:], func=ACT.Square)
@@ -266,7 +269,7 @@ def tile_list_wavefront_mode_scores_kernel(
         def root_pair(u, j0, j1):
             nc.scalar.activation(
                 out=zb[:].rearrange("p (j t) -> p j t", t=4)[:, j0:j1, 2 * u : 2 * u + 2],
-                in_=qt_flat[u][:].rearrange("p (t j) -> p j t", t=2)[:, j0:j1, :], func=ACT.Sqrt,
+                in_=raw[2][:].rearrange("p (t j) -> p j t", t=2)[:, j0:j1, :], func=ACT.Sqrt,
             )
 
         def quantize_z(a, j0, j1):
@@ -321,7 +324,7 @@ def tile_list_wavefront_mode_scores_kernel(
         for g in range(2):
             nc.vector.tensor_copy(vw[g][:], tabw[g][:].indirect(list1[:]))
         for i in range(2):
-            cast(i, raw[i], False)
+            cast(grouped[i][:], raw[i], False)
             quantize(w1c[i][:], w1s[i][:], grouped[i][:])
         wind_square(0)
         wind_square(1)
@@ -337,7 +340,7 @@ def tile_list_wavefront_mode_scores_kernel(
         scatter_a(0)
         wind_square(2)
         for i in (2, 3):
-            cast(i, raw[i], True)
+            cast(grouped[i][:], raw[i], True)
             quantize(w1c[i][:], w1s[i][:], grouped[i][:])
             load_rows(raw[i], wb, i - 2, 0)
         scatter_a(1)
@@ -366,9 +369,6 @@ def tile_list_wavefront_mode_scores_kernel(
         quantize_z(0, 0, T2)
         scatter_a(5)
         for s in range(4, 7):
-            if s < 6:
-                cast(s - 4, raw[s - 2], False)
-                quantize(wbc[s - 4][:], wbs[s - 4][:], grouped[s - 4][:])
             square_b(s)
             slope_square(s)
             turn_back(s)
@@ -377,28 +377,33 @@ def tile_list_wavefront_mode_scores_kernel(
             if s < 6:
                 slope_gain(s + 2)
                 scatter_a(s + 2)
+                values = slope4[1][:, S * (s - 3) : S * (s - 1)].bitcast(BF16)
+                cast(values, raw[s - 2], False)
+                quantize(wbc[s - 4][:], wbs[s - 4][:], values)
         wind_features(7, 4)
         scatter_b(7)
-        for h in range(2):
-            root_pair(0, 512 * h, 512 * (h + 1))
-        score_pass(0, 0, 0, 512, True, False)
+        for m in range(4):
+            nc.scalar.activation(
+                out=zb[:].rearrange("p (h j t) -> p h j t", h=2, t=4)[:, :, P * m : P * (m + 1), 0:2],
+                in_=st_flat[1][:].rearrange("p (t h j) -> p h j t", t=2, h=2)[:, :, P * m : P * (m + 1), :],
+                func=ACT.Sqrt,
+            )
         slope_square(7)
         turn_back(7)
+        score_pass(0, 0, 0, 512, True, False)
         score_pass(1, 0, 0, 512, True, False)
         score_pass(2, 0, 0, 512, True, False)
-        last_page = wind_page(7)
-        for h in range(2):
-            for j0 in (512 * h, 512 * h + 256):
-                nc.vector.tensor_tensor(
-                    zsq(7)[:, j0 : j0 + 256], last_page[:, j0 : j0 + 256], last_page[:, j0 : j0 + 256], ALU.mult
-                )
-            for j0 in (512 * h, 512 * h + 256):
-                add_squares(7, j0, j0 + 256)
-                root_pair(1, j0, j0 + 256)
-            if h == 1:
-                score_pass(3, 0, 0, 512, True, False)
-            for j0 in (512 * h, 512 * h + 256):
-                quantize_z(1, j0, j0 + 256)
+        for j0 in range(0, T2, 256):
+            h = j0 // 512
+            if j0 % 512 == 0:
+                nc.scalar.activation(out=turned(7, h), in_=wind_page(7)[:, j0 : j0 + 512], func=ACT.Square)
+            square = turned(7, h)[:, j0 - 512 * h : j0 - 512 * h + 256]
+            nc.vector.tensor_tensor(
+                zsq(7)[:, j0 : j0 + 256], back_bank(7, h)[:, j0 - 512 * h : j0 - 512 * h + 256], square, ALU.add
+            )
+            root_pair(1, j0, j0 + 256)
+            quantize_z(1, j0, j0 + 256)
+        score_pass(3, 0, 0, 512, True, False)
         for j0 in (0, 256):
             for i in range(4):
                 score_pass(i, 1, j0, j0 + 256, False, j0 == 256)

@@ -21,6 +21,7 @@ S = 512
 T2 = 1024
 TA = 2048
 TB = 1024
+Q = 256
 
 
 def tile_list_wavefront_mode_scores_kernel(
@@ -31,6 +32,7 @@ def tile_list_wavefront_mode_scores_kernel(
     with ExitStack() as ctx:
         lists = ctx.enter_context(tc.tile_pool(name="lists", bufs=1))
         keep = ctx.enter_context(tc.tile_pool(name="keep", bufs=1))
+        shared = ctx.enter_context(tc.tile_pool(name="shared", bufs=1))
         psum = ctx.enter_context(tc.psum_pool(name="psum", bufs=1))
 
         def sb(name, shape, dtype, tag=None):
@@ -44,22 +46,22 @@ def tile_list_wavefront_mode_scores_kernel(
 
         ident = sb("ident", [P, P], F32)
         tabw = [sb("tabw%d" % g, [P, TA], U32, tag="big%d" % g) for g in range(2)]
-        tabs = sb("tabs", [P, TA], U8)
-        tab2w = sb("tab2w", [P, TB], U32)
+        tabs = shared.tile([P, TA], U8, name="tabs", offset=0, align_bytes=64)
+        tab2w = shared.tile([P, TB], U32, name="tab2w", offset=36 * T2, align_bytes=64)
         tab2s = sb("tab2s", [P, TB], U8)
         vw = [sb("vw%d" % g, [P, S], U32) for g in range(2)]
         vs = sb("vs", [P, S], U8)
         v2w = sb("v2w", [P, S], U32)
         v2s = sb("v2s", [P, S], U8)
-        w2w = sb("w2w", [P, 1024], U32)
+        w2w = shared.tile([P, 1024], U32, name="w2w", offset=32 * T2, align_bytes=64)
         w2s = sb("w2s", [P, 1024], U8)
         w2w_dealt = sb("w2w_dealt", [P, 512], U32)
         w2s_dealt = sb("w2s_dealt", [P, 512], U8)
-        raw = [sb("raw%d" % i, [P, 2048], F32) for i in range(4)]
+        raw = [shared.tile([P, 2048], F32, name="raw0", offset=12 * T2, align_bytes=64)]
+        raw += [sb("raw%d" % i, [P, 2048], F32) for i in range(1, 4)]
         grouped = [sb("grouped%d" % i, [P, 2048], BF16) for i in range(4)]
         w1c = [sb("w1c%d" % i, [P, 512], U32) for i in range(4)]
         w1s = [sb("w1s%d" % i, [P, 512], U8) for i in range(4)]
-        wbc = [sb("wbc%d" % i, [P, 512], U32) for i in range(2)]
         wbs = [sb("wbs%d" % i, [P, 512], U8) for i in range(2)]
         waw = sb("waw", [P, 2048], U8)
         was = sb("was", [P, 1024], U8)
@@ -70,19 +72,20 @@ def tile_list_wavefront_mode_scores_kernel(
         wind4 = [sb("wind4_%d" % a, [P, 4 * S], F32) for a in range(2)]
         th = [slope4[s // 4][:, S * (s % 4) : S * (s % 4 + 1)] for s in range(8)]
         hw = [wind4[s // 4][:, S * (s % 4) : S * (s % 4 + 1)] for s in range(8)]
+        for s in range(2):
+            th[4 + s] = shared.tile([P, S], F32, name="th%d" % (4 + s), offset=28 * T2 + 4 * S * s, align_bytes=64)[:]
+            hw[s] = shared.tile([P, S], F32, name="hw%d" % s, offset=4 * T2 * (s + 1), align_bytes=64)[:]
+        gained4 = sb("gained4", [P, 4 * S], F32)
         ref = [sb("ref%d" % i, [P, T2], F32) for i in range(4)]
-        page_a = [sb("page_a%d" % i, [P, T2], F32) for i in range(4)]
-        page_b = [sb("page_b%d" % i, [P, T2], F32) for i in range(4)]
-        qt_second = sb("qt_second", [P, 2048], F32)
-        qt_flat = (raw[0], qt_second)
-        qt = [half[:].rearrange("p (c t r) -> p c t r", c=4, t=4) for half in qt_flat]
+        page_a = [sb("page_a0", [P, T2], F32)]
+        page_b = [sb("page_b%d" % i, [P, T2], F32) for i in range(3)]
         zb = sb("zb", [P, 4 * T2], BF16)
         zc = [sb("zc%d" % a, [P, T2], U32) for a in range(2)]
         zs = [sb("zs%d" % a, [P, T2], U8) for a in range(2)]
 
         for plane in (tab2s, w2s, was):
             nc.vector.memset(plane[:].bitcast(I32), 0)
-        for page in page_b[:2]:
+        for page in page_b + page_a:
             nc.vector.memset(page[:], 0.0)
 
         nc.gpsimd.memset(tabs[:].bitcast(I32), 0)
@@ -129,15 +132,14 @@ def tile_list_wavefront_mode_scores_kernel(
         load_words(tabw[0], tab_words[0])
         load_words(tabw[1], tab_words[1])
         load_rows(raw[1], w1, 1, 0)
-        nc.sync.dma_start(list3[:], offs3)
+        nc.sync.dma_start(out=wg1n[:], in_=wg1)
         with nc.allow_non_contiguous_dma(reason="one gain a partition"):
             nc.sync.dma_start(out=gain[0][:], in_=gain1[0:512].rearrange("(b p) -> p b", p=P))
         nc.sync.dma_start(out=gain[1][:], in_=gain1[512:1024].rearrange("(p t) -> p t", t=4))
-        nc.sync.dma_start(out=wg1n[:], in_=wg1)
-        load_ref(0)
+        nc.sync.dma_start(list3[:], offs3)
         load_rows(raw[2], w1, 0, 1)
         load_rows(raw[3], w1, 1, 1)
-        for s in range(1, 4):
+        for s in range(4):
             load_ref(s)
         for q in range(4):
             nc.sync.dma_start(
@@ -151,8 +153,6 @@ def tile_list_wavefront_mode_scores_kernel(
 
 
         make_identity(nc, ident[:])
-        for page in page_b[2:] + page_a:
-            nc.gpsimd.memset(page[:], 0.0)
 
         def cast(values, rows, dealt):
             if dealt:
@@ -185,60 +185,51 @@ def tile_list_wavefront_mode_scores_kernel(
                 )
             nc.scalar.activation(out=th[s], in_=bank[b][:], func=ACT.Tanh)
 
-        def slope_source(s):
-            return th[s] if s < 6 else turned(s - 2, 1)
+        def slope_weight(s):
+            if s < 4:
+                return gained4[:, S * s : S * (s + 1)]
+            return th[s - 4] if s < 6 else ref[s - 6][:, 0:S]
 
         def wind_source(s):
-            return raw[1][:, 0:S] if s == 3 else turned(6, 1) if s == 7 else hw[s]
+            return raw[1][:, 0:S] if s == 3 else ref[2][:, 0:S] if s == 7 else hw[s]
 
         def slope_gain(s):
             nc.scalar.activation(
-                out=slope_source(s), in_=th[s], func=ACT.Copy, scale=gain[s // 4][:, s % 4 : s % 4 + 1]
+                out=slope_weight(s), in_=wg1n[:] if s < 4 else th[s - 4], func=ACT.Copy,
+                scale=gain[s // 4][:, s % 4 : s % 4 + 1]
             )
 
         def slope_page(s):
             return page_a[s if s < 4 else s % 2]
 
         def scatter_a(s):
-            wg = wg1n[:] if s < 4 else th[s % 4]
-            nc.vector.tensor_tensor(slope_page(s)[:].indirect(list3[:]), slope_source(s), wg, ALU.mult)
+            nc.vector.tensor_tensor(slope_page(s)[:].indirect(list3[:]), th[s], slope_weight(s), ALU.mult)
 
         def wind_page(s):
-            return page_b[(s + s // 4 * 3) % 4]
+            return page_b[s % 3]
 
         def scatter_b(s):
-            wg = wg2n[:] if s < 4 else raw[1][:, S * (s % 4) : S * (s % 4 + 1)]
+            wg = wg2n[:] if s < 4 else wg2_dealt[:, S * (s % 4) : S * (s % 4 + 1)]
             nc.vector.tensor_tensor(wind_page(s)[:].indirect(list4[:]), wind_source(s), wg, ALU.mult)
 
         def turn(dst, src, start, stop):
             nc.tensor.matmul(dst, src, ident[:], start=start, stop=stop, is_transpose=True)
 
-        def turned(s, h):
-            return qt_flat[h][:, S * (s % 4) : S * (s % 4 + 1)]
-
-        def back_bank(s, h):
-            return bank[(2, 6, 2, 4)[s % 4] + h]
-
-        def turn_square(s, terms, b0, dst):
+        def turn_square(s, terms, banks, dst):
             for h in range(2):
-                b = bank[b0 + h]
+                b = bank[banks[h]]
                 for n, term in enumerate(terms):
                     for c in range(4):
                         j0 = 512 * h + P * c
                         turn(b[:, P * c : P * (c + 1)], term[:, j0 : j0 + P],
                              n == 0 and c == 0, n == len(terms) - 1 and c == 3)
-                if s < 4:
-                    nc.scalar.activation(
-                        out=dst[h][:, :, :, 32 * s : 32 * (s + 1)],
-                        in_=b[:].rearrange("p (c q t) -> p c t q", c=4, t=4), func=ACT.Square,
-                    )
-                else:
-                    nc.scalar.activation(
-                        out=turned(s, h), in_=b[:], func=ACT.Square
-                    )
+                nc.scalar.activation(
+                    out=dst[h][:, :, :, 32 * s : 32 * (s + 1)],
+                    in_=b[:].rearrange("p (c q t) -> p c t q", c=4, t=4), func=ACT.Square,
+                )
 
         def magnitude_turned(jc):
-            b = bank[(2 + jc) % 8]
+            b = bank[(4 + jc) % 8]
             for n, term in enumerate((qt, st)):
                 for t in range(4):
                     turn(b[:, P * t : P * (t + 1)], term[jc // 4][:, jc % 4, t, :],
@@ -250,21 +241,22 @@ def tile_list_wavefront_mode_scores_kernel(
 
         def zsq(s):
             t = s % 4
-            return (st_flat[1], raw[2])[t // 2][:, T2 * (t % 2) : T2 * (t % 2 + 1)]
+            return (first_pair, raw[2])[t // 2][:, T2 * (t % 2) : T2 * (t % 2 + 1)]
 
         def square_b(s):
             nc.scalar.activation(out=zsq(s), in_=wind_page(s)[:], func=ACT.Square)
 
-        def turn_back(s):
-            for h in range(2):
-                for c in range(4):
-                    turn(back_bank(s, h)[:, P * c : P * (c + 1)], turned(s, h)[:, P * c : P * (c + 1)], True, True)
+        def add_reference(s):
+            nc.vector.tensor_tensor(ref[s % 4][:], slope_page(s)[:], ref[s % 4][:], ALU.add)
+
+        def squared(s):
+            return ref[s % 4 if s < 6 else s - 6]
+
+        def square_a(s):
+            nc.scalar.activation(out=squared(s)[:], in_=ref[s % 4][:], func=ACT.Square)
 
         def add_squares(s, j0, j1):
-            h = j0 // 512
-            nc.vector.tensor_tensor(
-                zsq(s)[:, j0:j1], back_bank(s, h)[:, j0 - 512 * h : j1 - 512 * h], zsq(s)[:, j0:j1], ALU.add
-            )
+            nc.vector.tensor_tensor(zsq(s)[:, j0:j1], squared(s)[:, j0:j1], zsq(s)[:, j0:j1], ALU.add)
 
         def root_pair(u, j0, j1):
             nc.scalar.activation(
@@ -275,36 +267,37 @@ def tile_list_wavefront_mode_scores_kernel(
         def quantize_z(a, j0, j1):
             quantize(zc[a][:, j0:j1], zs[a][:, j0:j1], zb[:, 4 * j0 : 4 * j1])
 
-        pair_banks = (6, 2, 0, 4)
+        def score_bank(i, q):
+            return bank[4 * (q % 2) + i]
 
-        def score_pass(i, a, j0, j1, start, stop, which=(0, 1)):
-            h = j0 // 512
+        def score_pass(i, a, q):
             cols = slice(P * i, P * (i + 1))
+            slots = slice(Q * q, Q * (q + 1))
             stationary = (
                 (waw[:, 1024 * a + 256 * i : 1024 * a + 256 * (i + 1)].bitcast(FP4X4),
                  was[:, 512 * a + P * i : 512 * a + P * (i + 1)]),
                 (wbc[a][:, cols].bitcast(FP8X4), wbs[a][:, cols]),
             )
-            for n in which:
-                codes, scales = stationary[n]
+            for n, (codes, scales) in enumerate(stationary):
                 nc.tensor.matmul_mx(
-                    out=bank[pair_banks[i] + n][:, j0 - 512 * h : j1 - 512 * h], lhsT=codes, lhsT_scale=scales,
-                    rhs=zc[a][:, j0:j1].bitcast(FP8X4), rhs_scale=zs[a][:, j0:j1], start=start, stop=stop,
+                    out=score_bank(i, q)[:, Q * n : Q * (n + 1)], lhsT=codes, lhsT_scale=scales,
+                    rhs=zc[a][:, slots].bitcast(FP8X4), rhs_scale=zs[a][:, slots],
+                    start=(a == 0 and n == 0), stop=(a == 1 and n == 1),
                 )
 
-        def larger_score(i, h):
-            first, result = th[i], th[4 + i]
-            nc.scalar.copy(out=first, in_=bank[pair_banks[i]][:])
-            nc.vector.tensor_tensor(result, bank[pair_banks[i] + 1][:], first, ALU.max)
-            nc.sync.dma_start(out=out[P * i : P * (i + 1), 512 * h : 512 * (h + 1)], in_=result)
+        def larger_score(i, q):
+            first = slope4[0][:, Q * (4 * (q % 2) + i) : Q * (4 * (q % 2) + i + 1)]
+            result = wind4[q // 2][:, S * i + Q * (q % 2) : S * i + Q * (q % 2 + 1)]
+            nc.scalar.copy(out=first, in_=score_bank(i, q)[:, 0:Q])
+            nc.vector.tensor_tensor(result, score_bank(i, q)[:, Q : 2 * Q], first, ALU.max)
+            nc.sync.dma_start(out=out[P * i : P * (i + 1), Q * q : Q * (q + 1)], in_=result)
 
         def slope_square(s):
-            turn_square(s, (ref[s % 4], slope_page(s)), 0, st)
-            if s < 4:
-                load_ref(s + 4)
+            turn_square(s, (ref[s], page_a[s]), ((1, 4), (6, 7), (0, 2), (3, 1))[s], st)
+            load_ref(s + 4)
 
         def wind_square(s):
-            turn_square(s, (page_b[s],), 0, qt)
+            turn_square(s, (wind_page(s),), ((0, 1), (2, 1), (0, 5), (2, 3))[s], qt)
 
         nc.vector.tensor_copy(v2w[:], tab2w[:].indirect(list2[:]))
         nc.vector.tensor_copy(v2s[:], tab2s[:].indirect(list2[:]))
@@ -319,98 +312,95 @@ def tile_list_wavefront_mode_scores_kernel(
         for s in range(3):
             wind_features(s, 4 + s)
             scatter_b(s)
-        for s in range(4, 7):
-            wind_features(s, s - 2)
+        for i in range(1, 4):
+            page_a.append(shared.tile([P, T2], F32, name="page_a%d" % i, offset=4 * T2 * (i - 1), align_bytes=64))
+            nc.gpsimd.memset(page_a[i][:], 0.0)
         for g in range(2):
             nc.vector.tensor_copy(vw[g][:], tabw[g][:].indirect(list1[:]))
         for i in range(2):
             cast(grouped[i][:], raw[i], False)
             quantize(w1c[i][:], w1s[i][:], grouped[i][:])
+        qt_whole = shared.tile([P, 4096], F32, name="qt_whole", offset=12 * T2, align_bytes=64)
+        qt = [qt_whole[:, 2048 * h : 2048 * (h + 1)].rearrange("p (c t r) -> p c t r", c=4, t=4) for h in range(2)]
         wind_square(0)
         wind_square(1)
         wind_features(3, 1)
         scatter_b(3)
-        load_dealt(raw[1], wg2)
+        wg2_dealt = shared.tile([P, 4 * S], F32, name="wg2_dealt", offset=32 * T2, align_bytes=64)
+        load_dealt(wg2_dealt, wg2)
         st_flat = [sb("st%d" % h, [P, 4 * S], F32, tag="big%d" % h) for h in range(2)]
         st = [half[:].rearrange("p (c t r) -> p c t r", c=4, t=4) for half in st_flat]
-        slope_tanh(0, 0)
-        slope_gain(0)
-        slope_tanh(1, 5)
-        slope_gain(1)
-        scatter_a(0)
-        wind_square(2)
+        for s in range(4):
+            slope_gain(s)
+        for s in range(4):
+            slope_tanh(s, (0, 5, 6, 7)[s])
+            scatter_a(s)
         for i in (2, 3):
             cast(grouped[i][:], raw[i], True)
             quantize(w1c[i][:], w1s[i][:], grouped[i][:])
             load_rows(raw[i], wb, i - 2, 0)
-        scatter_a(1)
-        slope_tanh(2, 6)
-        slope_gain(2)
-        slope_tanh(3, 7)
-        slope_gain(3)
-        scatter_a(2)
-        scatter_a(3)
         load_dealt(slope4[0], wg1)
-        slope_square(0)
+        wind_square(2)
         wind_square(3)
-        slope_square(1)
-        for s in range(4, 8):
-            slope_tanh(s, s)
+        for s in range(4, 7):
+            wind_features(s, 5)
+        for s in range(4):
+            slope_square(s)
         slope_gain(4)
         slope_gain(5)
-        scatter_b(4)
-        slope_square(2)
-        slope_square(3)
-        scatter_b(5)
-        scatter_b(6)
+        for s in range(4, 8):
+            slope_tanh(s, (0, 2, 3, 1)[s - 4])
+        for a in range(2):
+            cast(grouped[a][:], raw[2 + a], False)
+        for s in range(4, 7):
+            scatter_b(s)
+        first_pair = shared.tile([P, 2 * T2], F32, name="first_pair", offset=4 * T2, align_bytes=64)
+        for s in (4, 5):
+            scatter_a(s)
+        for s in (4, 5):
+            add_reference(s)
+            square_b(s)
+            square_a(s)
+        wbc = [
+            shared.tile([P, 512], U32, name="wbc%d" % a, offset=28 * T2 + 4 * S * a, align_bytes=64) for a in range(2)
+        ]
+        for a in range(2):
+            quantize(wbc[a][:], wbs[a][:], grouped[a][:])
+        for s in (4, 5):
+            add_squares(s, 0, T2)
+            slope_gain(s + 2)
+            scatter_a(s + 2)
         for jc in range(8):
             magnitude_turned(jc)
-        scatter_a(4)
         quantize_z(0, 0, T2)
-        scatter_a(5)
-        for s in range(4, 7):
-            square_b(s)
-            slope_square(s)
-            turn_back(s)
-            for h in range(2):
-                add_squares(s, 512 * h, 512 * (h + 1))
-            if s < 6:
-                slope_gain(s + 2)
-                scatter_a(s + 2)
-                values = slope4[1][:, S * (s - 3) : S * (s - 1)].bitcast(BF16)
-                cast(values, raw[s - 2], False)
-                quantize(wbc[s - 4][:], wbs[s - 4][:], values)
-        wind_features(7, 4)
+        add_reference(6)
+        add_reference(7)
+        square_b(6)
+        square_a(6)
+        add_squares(6, 0, T2)
+        wind_features(7, 7)
         scatter_b(7)
-        for m in range(4):
+        square_a(7)
+        for h in range(2):
             nc.scalar.activation(
-                out=zb[:].rearrange("p (h j t) -> p h j t", h=2, t=4)[:, :, P * m : P * (m + 1), 0:2],
-                in_=st_flat[1][:].rearrange("p (t h j) -> p h j t", t=2, h=2)[:, :, P * m : P * (m + 1), :],
+                out=zb[:].rearrange("p (j t) -> p j t", t=4)[:, 512 * h : 512 * (h + 1), 0:2],
+                in_=first_pair[:].rearrange("p (t j) -> p j t", t=2)[:, 512 * h : 512 * (h + 1), :],
                 func=ACT.Sqrt,
             )
-        slope_square(7)
-        turn_back(7)
-        score_pass(0, 0, 0, 512, True, False)
-        score_pass(1, 0, 0, 512, True, False)
-        score_pass(2, 0, 0, 512, True, False)
-        for j0 in range(0, T2, 256):
-            h = j0 // 512
-            if j0 % 512 == 0:
-                nc.scalar.activation(out=turned(7, h), in_=wind_page(7)[:, j0 : j0 + 512], func=ACT.Square)
-            square = turned(7, h)[:, j0 - 512 * h : j0 - 512 * h + 256]
-            nc.vector.tensor_tensor(
-                zsq(7)[:, j0 : j0 + 256], back_bank(7, h)[:, j0 - 512 * h : j0 - 512 * h + 256], square, ALU.add
-            )
-            root_pair(1, j0, j0 + 256)
-            quantize_z(1, j0, j0 + 256)
-        score_pass(3, 0, 0, 512, True, False)
-        for j0 in (0, 256):
+        for q in range(2):
             for i in range(4):
-                score_pass(i, 1, j0, j0 + 256, False, j0 == 256)
-        for i in range(4):
-            larger_score(i, 0)
-            for n in range(2):
-                score_pass(i, 0, 512, 1024, True, False, (n,))
-                score_pass(i, 1, 512, 1024, False, True, (n,))
-        for i in range(4):
-            larger_score(i, 1)
+                score_pass(i, 0, q)
+        last = wind_page(7)
+        nc.vector.tensor_tensor(zsq(7)[:, 0:Q], last[:, 0:Q], last[:, 0:Q], ALU.mult)
+        nc.scalar.activation(out=zsq(7)[:, Q:T2], in_=last[:, Q:T2], func=ACT.Square)
+        for q in range(4):
+            j0 = Q * q
+            add_squares(7, j0, j0 + Q)
+            root_pair(1, j0, j0 + Q)
+            quantize_z(1, j0, j0 + Q)
+        for q in range(4):
+            for i in range(4):
+                if q >= 2:
+                    score_pass(i, 0, q)
+                score_pass(i, 1, q)
+                larger_score(i, q)

@@ -47,19 +47,23 @@ def tile_list_wavefront_mode_scores_kernel(
         ident = sb("ident", [P, P], F32)
         tabw = [sb("tabw%d" % g, [P, TA], U32, tag="big%d" % g) for g in range(2)]
         tabs = shared.tile([P, TA], U8, name="tabs", offset=0, align_bytes=64)
-        tab2w = shared.tile([P, TB], U32, name="tab2w", offset=36 * T2, align_bytes=64)
+        tab2w = sb("tab2w", [P, TB], U32)
         tab2s = sb("tab2s", [P, TB], U8)
         vw = [sb("vw%d" % g, [P, S], U32) for g in range(2)]
         vs = sb("vs", [P, S], U8)
         v2w = sb("v2w", [P, S], U32)
         v2s = sb("v2s", [P, S], U8)
-        w2w = shared.tile([P, 1024], U32, name="w2w", offset=32 * T2, align_bytes=64)
+        w2w = sb("w2w", [P, 1024], U32)
         w2s = sb("w2s", [P, 1024], U8)
         w2w_dealt = sb("w2w_dealt", [P, 512], U32)
         w2s_dealt = sb("w2s_dealt", [P, 512], U8)
-        raw = [shared.tile([P, 2048], F32, name="raw0", offset=12 * T2, align_bytes=64)]
+        raw = [shared.tile([P, 2048], F32, name="raw0", offset=20 * T2, align_bytes=64)]
         raw += [sb("raw%d" % i, [P, 2048], F32) for i in range(1, 4)]
-        grouped = [sb("grouped%d" % i, [P, 2048], BF16) for i in range(4)]
+        grouped = [
+            shared.tile([P, 2048], BF16, name="grouped%d" % i, offset=(40 + 4 * i) * T2, align_bytes=64)
+            for i in range(2)
+        ]
+        grouped += [sb("grouped%d" % i, [P, 2048], BF16) for i in range(2, 6)]
         w1c = [sb("w1c%d" % i, [P, 512], U32) for i in range(4)]
         w1s = [sb("w1s%d" % i, [P, 512], U8) for i in range(4)]
         wbs = [sb("wbs%d" % i, [P, 512], U8) for i in range(2)]
@@ -73,19 +77,19 @@ def tile_list_wavefront_mode_scores_kernel(
         th = [slope4[s // 4][:, S * (s % 4) : S * (s % 4 + 1)] for s in range(8)]
         hw = [wind4[s // 4][:, S * (s % 4) : S * (s % 4 + 1)] for s in range(8)]
         for s in range(2):
-            th[4 + s] = shared.tile([P, S], F32, name="th%d" % (4 + s), offset=28 * T2 + 4 * S * s, align_bytes=64)[:]
-            hw[s] = shared.tile([P, S], F32, name="hw%d" % s, offset=4 * T2 * (s + 1), align_bytes=64)[:]
+            th[4 + s] = shared.tile([P, S], F32, name="th%d" % (4 + s), offset=36 * T2 + 4 * S * s, align_bytes=64)[:]
+            hw[s] = shared.tile([P, S], F32, name="hw%d" % s, offset=(7 + 8 * s) * T2, align_bytes=64)[:]
         gained4 = sb("gained4", [P, 4 * S], F32)
         ref = [sb("ref%d" % i, [P, T2], F32) for i in range(4)]
-        page_a = [sb("page_a0", [P, T2], F32)]
-        page_b = [sb("page_b%d" % i, [P, T2], F32) for i in range(3)]
+        page_a = []
+        page_b = [sb("page_b%d" % i, [P, T2], F32) for i in range(2)]
         zb = sb("zb", [P, 4 * T2], BF16)
         zc = [sb("zc%d" % a, [P, T2], U32) for a in range(2)]
         zs = [sb("zs%d" % a, [P, T2], U8) for a in range(2)]
 
         for plane in (tab2s, w2s, was):
             nc.vector.memset(plane[:].bitcast(I32), 0)
-        for page in page_b + page_a:
+        for page in page_b:
             nc.vector.memset(page[:], 0.0)
 
         nc.gpsimd.memset(tabs[:].bitcast(I32), 0)
@@ -141,16 +145,6 @@ def tile_list_wavefront_mode_scores_kernel(
         load_rows(raw[3], w1, 1, 1)
         for s in range(4):
             load_ref(s)
-        for q in range(4):
-            nc.sync.dma_start(
-                out=was[32 * q : 32 * q + 4, :].bitcast(I32).rearrange("p (a n) -> p a n", a=2),
-                in_=wa_scales[:, 4 * q : 4 * q + 4, :].bitcast(I32).rearrange("a r n -> r a n"),
-            )
-        nc.sync.dma_start(
-            out=waw[:].bitcast(I32).rearrange("p (a c) -> p a c", a=2),
-            in_=wa_words.bitcast(I32).rearrange("a p c -> p a c"),
-        )
-
 
         make_identity(nc, ident[:])
 
@@ -186,21 +180,19 @@ def tile_list_wavefront_mode_scores_kernel(
             nc.scalar.activation(out=th[s], in_=bank[b][:], func=ACT.Tanh)
 
         def slope_weight(s):
-            if s < 4:
-                return gained4[:, S * s : S * (s + 1)]
-            return th[s - 4] if s < 6 else ref[s - 6][:, 0:S]
+            return (gained4, raw[1])[s // 4][:, S * (s % 4) : S * (s % 4 + 1)]
 
         def wind_source(s):
-            return raw[1][:, 0:S] if s == 3 else ref[2][:, 0:S] if s == 7 else hw[s]
+            return raw[1][:, 0:S] if s == 3 else hw[s]
 
         def slope_gain(s):
             nc.scalar.activation(
-                out=slope_weight(s), in_=wg1n[:] if s < 4 else th[s - 4], func=ACT.Copy,
+                out=slope_weight(s) if s < 4 else th[s], in_=wg1n[:] if s < 4 else th[s], func=ACT.Copy,
                 scale=gain[s // 4][:, s % 4 : s % 4 + 1]
             )
 
         def slope_page(s):
-            return page_a[s if s < 4 else s % 2]
+            return page_a[s % 4]
 
         def scatter_a(s):
             nc.vector.tensor_tensor(slope_page(s)[:].indirect(list3[:]), th[s], slope_weight(s), ALU.mult)
@@ -223,13 +215,17 @@ def tile_list_wavefront_mode_scores_kernel(
                         j0 = 512 * h + P * c
                         turn(b[:, P * c : P * (c + 1)], term[:, j0 : j0 + P],
                              n == 0 and c == 0, n == len(terms) - 1 and c == 3)
-                nc.scalar.activation(
-                    out=dst[h][:, :, :, 32 * s : 32 * (s + 1)],
-                    in_=b[:].rearrange("p (c q t) -> p c t q", c=4, t=4), func=ACT.Square,
-                )
+                if s < 4:
+                    nc.scalar.activation(
+                        out=dst[h][:, :, :, 32 * s : 32 * (s + 1)],
+                        in_=b[:].rearrange("p (c q t) -> p c t q", c=4, t=4), func=ACT.Square,
+                    )
+                else:
+                    j0 = T2 * (s - 4) + 512 * h
+                    nc.scalar.activation(out=dst[:, j0 : j0 + 512], in_=b[:], func=ACT.Square)
 
         def magnitude_turned(jc):
-            b = bank[(4 + jc) % 8]
+            b = bank[(4, 5, 6, 7, 0, 2, 3, 1)[jc]]
             for n, term in enumerate((qt, st)):
                 for t in range(4):
                     turn(b[:, P * t : P * (t + 1)], term[jc // 4][:, jc % 4, t, :],
@@ -239,24 +235,33 @@ def tile_list_wavefront_mode_scores_kernel(
                 in_=b[:].rearrange("p (t j) -> p j t", t=4), func=ACT.Sqrt,
             )
 
-        def zsq(s):
-            t = s % 4
-            return (first_pair, raw[2])[t // 2][:, T2 * (t % 2) : T2 * (t % 2 + 1)]
+        def magnitude_pair(q):
+            b = bank[(0, 2, 3, 1)[q]]
+            for n, term in enumerate((slope4[0], gained4)):
+                for t in range(2):
+                    for c in range(2):
+                        j0 = T2 * t + Q * q + P * c
+                        turn(b[:, Q * t + P * c : Q * t + P * (c + 1)], term[:, j0 : j0 + P],
+                             n == 0 and t == 0 and c == 0, n == 1 and t == 1 and c == 1)
+            nc.scalar.activation(
+                out=zb[:].rearrange("p (j t) -> p j t", t=4)[:, Q * q : Q * (q + 1), 0:2],
+                in_=b[:].rearrange("p (t j) -> p j t", t=2), func=ACT.Sqrt,
+            )
 
-        def square_b(s):
-            nc.scalar.activation(out=zsq(s), in_=wind_page(s)[:], func=ACT.Square)
+        def zsq(s):
+            return raw[2][:, T2 * (s - 6) : T2 * (s - 5)]
 
         def add_reference(s):
             nc.vector.tensor_tensor(ref[s % 4][:], slope_page(s)[:], ref[s % 4][:], ALU.add)
 
-        def squared(s):
-            return ref[s % 4 if s < 6 else s - 6]
-
         def square_a(s):
-            nc.scalar.activation(out=squared(s)[:], in_=ref[s % 4][:], func=ACT.Square)
+            nc.scalar.activation(out=zsq(s), in_=ref[s % 4][:], func=ACT.Square)
+
+        def square_b(s):
+            nc.scalar.activation(out=ref[s % 4][:], in_=wind_page(s)[:], func=ACT.Square)
 
         def add_squares(s, j0, j1):
-            nc.vector.tensor_tensor(zsq(s)[:, j0:j1], squared(s)[:, j0:j1], zsq(s)[:, j0:j1], ALU.add)
+            nc.vector.tensor_tensor(zsq(s)[:, j0:j1], ref[s % 4][:, j0:j1], zsq(s)[:, j0:j1], ALU.add)
 
         def root_pair(u, j0, j1):
             nc.scalar.activation(
@@ -293,11 +298,13 @@ def tile_list_wavefront_mode_scores_kernel(
             nc.sync.dma_start(out=out[P * i : P * (i + 1), Q * q : Q * (q + 1)], in_=result)
 
         def slope_square(s):
-            turn_square(s, (ref[s], page_a[s]), ((1, 4), (6, 7), (0, 2), (3, 1))[s], st)
-            load_ref(s + 4)
+            banks = ((1, 4), (6, 7), (0, 2), (3, 1), (4, 5), (6, 7))[s]
+            turn_square(s, (ref[s % 4], slope_page(s)), banks, st if s < 4 else gained4)
+            if s < 4:
+                load_ref(s + 4)
 
         def wind_square(s):
-            turn_square(s, (wind_page(s),), ((0, 1), (2, 1), (0, 5), (2, 3))[s], qt)
+            turn_square(s, (wind_page(s),), ((0, 1), (2, 1), (0, 5), (2, 3), (0, 2), (3, 1))[s], qt if s < 4 else slope4[0])
 
         nc.vector.tensor_copy(v2w[:], tab2w[:].indirect(list2[:]))
         nc.vector.tensor_copy(v2s[:], tab2s[:].indirect(list2[:]))
@@ -309,25 +316,30 @@ def tile_list_wavefront_mode_scores_kernel(
             w2s_dealt[:].rearrange("p (t m) -> p t m", t=4), w2s[:, 512:1024].rearrange("p (m t) -> p t m", t=4)
         )
         nc.vector.tensor_copy(vs[:], tabs[:].indirect(list1[:]))
+        page_b.append(shared.tile([P, T2], F32, name="page_b2", offset=0, align_bytes=64))
+        nc.gpsimd.memset(page_b[2][:], 0.0)
         for s in range(3):
             wind_features(s, 4 + s)
             scatter_b(s)
-        for i in range(1, 4):
-            page_a.append(shared.tile([P, T2], F32, name="page_a%d" % i, offset=4 * T2 * (i - 1), align_bytes=64))
+        for i in range(4):
+            page_a.append(shared.tile([P, T2], F32, name="page_a%d" % i, offset=4 * T2 * (i + 1), align_bytes=64))
             nc.gpsimd.memset(page_a[i][:], 0.0)
+        for s in range(4, 7):
+            wind_features(s, (2, 3, 7)[s - 4])
         for g in range(2):
             nc.vector.tensor_copy(vw[g][:], tabw[g][:].indirect(list1[:]))
         for i in range(2):
             cast(grouped[i][:], raw[i], False)
             quantize(w1c[i][:], w1s[i][:], grouped[i][:])
-        qt_whole = shared.tile([P, 4096], F32, name="qt_whole", offset=12 * T2, align_bytes=64)
+        qt_whole = shared.tile([P, 4096], F32, name="qt_whole", offset=20 * T2, align_bytes=64)
         qt = [qt_whole[:, 2048 * h : 2048 * (h + 1)].rearrange("p (c t r) -> p c t r", c=4, t=4) for h in range(2)]
         wind_square(0)
         wind_square(1)
         wind_features(3, 1)
         scatter_b(3)
-        wg2_dealt = shared.tile([P, 4 * S], F32, name="wg2_dealt", offset=32 * T2, align_bytes=64)
+        wg2_dealt = shared.tile([P, 4 * S], F32, name="wg2_dealt", offset=40 * T2, align_bytes=64)
         load_dealt(wg2_dealt, wg2)
+        load_dealt(raw[1], wg1)
         st_flat = [sb("st%d" % h, [P, 4 * S], F32, tag="big%d" % h) for h in range(2)]
         st = [half[:].rearrange("p (c t r) -> p c t r", c=4, t=4) for half in st_flat]
         for s in range(4):
@@ -339,60 +351,58 @@ def tile_list_wavefront_mode_scores_kernel(
             cast(grouped[i][:], raw[i], True)
             quantize(w1c[i][:], w1s[i][:], grouped[i][:])
             load_rows(raw[i], wb, i - 2, 0)
-        load_dealt(slope4[0], wg1)
+        for q in range(4):
+            nc.sync.dma_start(
+                out=was[32 * q : 32 * q + 4, :].bitcast(I32).rearrange("p (a n) -> p a n", a=2),
+                in_=wa_scales[:, 4 * q : 4 * q + 4, :].bitcast(I32).rearrange("a r n -> r a n"),
+            )
+        nc.sync.dma_start(
+            out=waw[:].bitcast(I32).rearrange("p (a c) -> p a c", a=2),
+            in_=wa_words.bitcast(I32).rearrange("a p c -> p a c"),
+        )
         wind_square(2)
         wind_square(3)
-        for s in range(4, 7):
-            wind_features(s, 5)
         for s in range(4):
+            if s >= 2:
+                cast(grouped[s + 2][:], raw[s], False)
             slope_square(s)
-        slope_gain(4)
-        slope_gain(5)
         for s in range(4, 8):
             slope_tanh(s, (0, 2, 3, 1)[s - 4])
-        for a in range(2):
-            cast(grouped[a][:], raw[2 + a], False)
+            slope_gain(s)
         for s in range(4, 7):
             scatter_b(s)
-        first_pair = shared.tile([P, 2 * T2], F32, name="first_pair", offset=4 * T2, align_bytes=64)
-        for s in (4, 5):
+        for s in (4, 6, 5):
             scatter_a(s)
-        for s in (4, 5):
-            add_reference(s)
-            square_b(s)
-            square_a(s)
-        wbc = [
-            shared.tile([P, 512], U32, name="wbc%d" % a, offset=28 * T2 + 4 * S * a, align_bytes=64) for a in range(2)
-        ]
-        for a in range(2):
-            quantize(wbc[a][:], wbs[a][:], grouped[a][:])
-        for s in (4, 5):
-            add_squares(s, 0, T2)
-            slope_gain(s + 2)
-            scatter_a(s + 2)
+        add_reference(6)
+        scatter_a(7)
+        wind_square(4)
+        wind_square(5)
         for jc in range(8):
             magnitude_turned(jc)
-        quantize_z(0, 0, T2)
-        add_reference(6)
-        add_reference(7)
-        square_b(6)
+        slope_square(4)
+        slope_square(5)
         square_a(6)
+        square_b(6)
+        add_reference(7)
+        wbc = [
+            shared.tile([P, 512], U32, name="wbc%d" % a, offset=36 * T2 + 4 * S * a, align_bytes=64) for a in range(2)
+        ]
+        for a in range(2):
+            quantize(wbc[a][:], wbs[a][:], grouped[4 + a][:])
+        quantize_z(0, 0, T2)
         add_squares(6, 0, T2)
+        hw[7] = shared.tile([P, S], F32, name="hw7", offset=16 * T2, align_bytes=64)[:]
         wind_features(7, 7)
         scatter_b(7)
         square_a(7)
-        for h in range(2):
-            nc.scalar.activation(
-                out=zb[:].rearrange("p (j t) -> p j t", t=4)[:, 512 * h : 512 * (h + 1), 0:2],
-                in_=first_pair[:].rearrange("p (t j) -> p j t", t=2)[:, 512 * h : 512 * (h + 1), :],
-                func=ACT.Sqrt,
-            )
+        for q in range(4):
+            magnitude_pair(q)
         for q in range(2):
             for i in range(4):
                 score_pass(i, 0, q)
         last = wind_page(7)
-        nc.vector.tensor_tensor(zsq(7)[:, 0:Q], last[:, 0:Q], last[:, 0:Q], ALU.mult)
-        nc.scalar.activation(out=zsq(7)[:, Q:T2], in_=last[:, Q:T2], func=ACT.Square)
+        nc.vector.tensor_tensor(ref[3][:, 0:Q], last[:, 0:Q], last[:, 0:Q], ALU.mult)
+        nc.scalar.activation(out=ref[3][:, Q:T2], in_=last[:, Q:T2], func=ACT.Square)
         for q in range(4):
             j0 = Q * q
             add_squares(7, j0, j0 + Q)

@@ -22,6 +22,7 @@ T2 = 1024
 TA = 2048
 TB = 1024
 Q = 256
+PIECES = ((0, 128), (128, 256), (256, 512), (512, 768), (768, 1024))
 
 
 def tile_list_wavefront_mode_scores_kernel(
@@ -80,11 +81,12 @@ def tile_list_wavefront_mode_scores_kernel(
             th[4 + s] = shared.tile([P, S], F32, name="th%d" % (4 + s), offset=36 * T2 + 4 * S * s, align_bytes=64)[:]
             hw[s] = shared.tile([P, S], F32, name="hw%d" % s, offset=(7 + 8 * s) * T2, align_bytes=64)[:]
         gained4 = sb("gained4", [P, 4 * S], F32)
-        ref = [sb("ref%d" % i, [P, T2], F32) for i in range(4)]
+        ref = [sb("ref%d" % i, [P, T2], F32) for i in range(3)]
+        ref.append(shared.tile([P, T2], F32, name="ref3", offset=48 * T2, align_bytes=64))
         page_a = []
         page_b = [sb("page_b%d" % i, [P, T2], F32) for i in range(2)]
-        zb = sb("zb", [P, 4 * T2], BF16)
-        zc = [sb("zc%d" % a, [P, T2], U32) for a in range(2)]
+        zb = [sb("zb%d" % a, [P, 4 * T2], BF16) for a in range(2)]
+        zc = [sb("zc0", [P, 512], U32), None, sb("zc2", [P, 512], U32), sb("zc3", [P, 512], U32)]
         zs = [sb("zs%d" % a, [P, T2], U8) for a in range(2)]
 
         for plane in (tab2s, w2s, was):
@@ -231,7 +233,7 @@ def tile_list_wavefront_mode_scores_kernel(
                     turn(b[:, P * t : P * (t + 1)], term[jc // 4][:, jc % 4, t, :],
                          n == 0 and t == 0, n == 1 and t == 3)
             nc.scalar.activation(
-                out=zb[:, 512 * jc : 512 * (jc + 1)].rearrange("p (j t) -> p j t", t=4),
+                out=zb[0][:, 512 * jc : 512 * (jc + 1)].rearrange("p (j t) -> p j t", t=4),
                 in_=b[:].rearrange("p (t j) -> p j t", t=4), func=ACT.Sqrt,
             )
 
@@ -244,7 +246,7 @@ def tile_list_wavefront_mode_scores_kernel(
                         turn(b[:, Q * t + P * c : Q * t + P * (c + 1)], term[:, j0 : j0 + P],
                              n == 0 and t == 0 and c == 0, n == 1 and t == 1 and c == 1)
             nc.scalar.activation(
-                out=zb[:].rearrange("p (j t) -> p j t", t=4)[:, Q * q : Q * (q + 1), 0:2],
+                out=zb[1][:].rearrange("p (j t) -> p j t", t=4)[:, Q * q : Q * (q + 1), 0:2],
                 in_=b[:].rearrange("p (t j) -> p j t", t=2), func=ACT.Sqrt,
             )
 
@@ -265,36 +267,39 @@ def tile_list_wavefront_mode_scores_kernel(
 
         def root_pair(u, j0, j1):
             nc.scalar.activation(
-                out=zb[:].rearrange("p (j t) -> p j t", t=4)[:, j0:j1, 2 * u : 2 * u + 2],
+                out=zb[1][:].rearrange("p (j t) -> p j t", t=4)[:, j0:j1, 2 * u : 2 * u + 2],
                 in_=raw[2][:].rearrange("p (t j) -> p j t", t=2)[:, j0:j1, :], func=ACT.Sqrt,
             )
 
+        def z_codes(a, j0, j1):
+            h = j0 // 512
+            return zc[2 * a + h][:, j0 - 512 * h : j1 - 512 * h]
+
         def quantize_z(a, j0, j1):
-            quantize(zc[a][:, j0:j1], zs[a][:, j0:j1], zb[:, 4 * j0 : 4 * j1])
+            quantize(z_codes(a, j0, j1), zs[a][:, j0:j1], zb[a][:, 4 * j0 : 4 * j1])
 
-        def score_bank(i, q):
-            return bank[4 * (q % 2) + i]
+        def score_sum(i, n, q):
+            b = bank[i if q == 3 and n == 0 else 4 * (q % 2) + i]
+            return b[:, Q * n : Q * (n + 1)]
 
-        def score_pass(i, a, q):
+        def score_pass(i, n, a, j0, j1, start, stop):
+            q = j0 // Q
             cols = slice(P * i, P * (i + 1))
-            slots = slice(Q * q, Q * (q + 1))
-            stationary = (
-                (waw[:, 1024 * a + 256 * i : 1024 * a + 256 * (i + 1)].bitcast(FP4X4),
-                 was[:, 512 * a + P * i : 512 * a + P * (i + 1)]),
-                (wbc[a][:, cols].bitcast(FP8X4), wbs[a][:, cols]),
+            if n == 0:
+                codes = waw[:, 1024 * a + 256 * i : 1024 * a + 256 * (i + 1)].bitcast(FP4X4)
+                scales = was[:, 512 * a + P * i : 512 * a + P * (i + 1)]
+            else:
+                codes, scales = wbc[a][:, cols].bitcast(FP8X4), wbs[a][:, cols]
+            nc.tensor.matmul_mx(
+                out=score_sum(i, n, q)[:, j0 - Q * q : j1 - Q * q], lhsT=codes, lhsT_scale=scales,
+                rhs=z_codes(a, j0, j1).bitcast(FP8X4), rhs_scale=zs[a][:, j0:j1], start=start, stop=stop,
             )
-            for n, (codes, scales) in enumerate(stationary):
-                nc.tensor.matmul_mx(
-                    out=score_bank(i, q)[:, Q * n : Q * (n + 1)], lhsT=codes, lhsT_scale=scales,
-                    rhs=zc[a][:, slots].bitcast(FP8X4), rhs_scale=zs[a][:, slots],
-                    start=(a == 0 and n == 0), stop=(a == 1 and n == 1),
-                )
 
         def larger_score(i, q):
             first = slope4[0][:, Q * (4 * (q % 2) + i) : Q * (4 * (q % 2) + i + 1)]
             result = wind4[q // 2][:, S * i + Q * (q % 2) : S * i + Q * (q % 2 + 1)]
-            nc.scalar.copy(out=first, in_=score_bank(i, q)[:, 0:Q])
-            nc.vector.tensor_tensor(result, score_bank(i, q)[:, Q : 2 * Q], first, ALU.max)
+            nc.scalar.copy(out=first, in_=score_sum(i, 0, q))
+            nc.vector.tensor_tensor(result, score_sum(i, 1, q), first, ALU.max)
             nc.sync.dma_start(out=out[P * i : P * (i + 1), Q * q : Q * (q + 1)], in_=result)
 
         def slope_square(s):
@@ -384,33 +389,45 @@ def tile_list_wavefront_mode_scores_kernel(
         square_a(6)
         square_b(6)
         add_reference(7)
-        wbc = [
-            shared.tile([P, 512], U32, name="wbc%d" % a, offset=36 * T2 + 4 * S * a, align_bytes=64) for a in range(2)
-        ]
-        for a in range(2):
-            quantize(wbc[a][:], wbs[a][:], grouped[4 + a][:])
-        quantize_z(0, 0, T2)
+        wbc = [shared.tile([P, 512], U32, name="wbc0", offset=36 * T2, align_bytes=64)]
+        quantize(wbc[0][:], wbs[0][:], grouped[4][:])
+        quantize_z(0, 0, 512)
         add_squares(6, 0, T2)
         hw[7] = shared.tile([P, S], F32, name="hw7", offset=16 * T2, align_bytes=64)[:]
-        wind_features(7, 7)
+        wind_features(7, 6)
         scatter_b(7)
         square_a(7)
         for q in range(4):
             magnitude_pair(q)
         for q in range(2):
             for i in range(4):
-                score_pass(i, 0, q)
+                for n in range(2):
+                    score_pass(i, n, 0, Q * q, Q * (q + 1), n == 0, False)
         last = wind_page(7)
-        nc.vector.tensor_tensor(ref[3][:, 0:Q], last[:, 0:Q], last[:, 0:Q], ALU.mult)
+        first_square = shared.tile([P, Q], F32, name="first_square", offset=38 * T2, align_bytes=64)
+        for j0, j1 in PIECES[:2]:
+            nc.vector.tensor_tensor(first_square[:, j0:j1], last[:, j0:j1], last[:, j0:j1], ALU.mult)
         nc.scalar.activation(out=ref[3][:, Q:T2], in_=last[:, Q:T2], func=ACT.Square)
-        for q in range(4):
-            j0 = Q * q
-            add_squares(7, j0, j0 + Q)
-            root_pair(1, j0, j0 + Q)
-            quantize_z(1, j0, j0 + Q)
-        for q in range(4):
+        for j0, j1 in PIECES:
+            square = first_square[:, j0:j1] if j0 < Q else ref[3][:, j0:j1]
+            nc.vector.tensor_tensor(zsq(7)[:, j0:j1], square, zsq(7)[:, j0:j1], ALU.add)
+            root_pair(1, j0, j1)
+            quantize_z(1, j0, j1)
+        wbc.append(shared.tile([P, 512], U32, name="wbc1", offset=38 * T2, align_bytes=64))
+        quantize(wbc[1][:], wbs[1][:], grouped[5][:])
+        zc[1] = shared.tile([P, 512], U32, name="zc1", offset=48 * T2, align_bytes=64)
+        quantize_z(0, 512, T2)
+        for j0, j1 in PIECES[:3]:
             for i in range(4):
-                if q >= 2:
-                    score_pass(i, 0, q)
-                score_pass(i, 1, q)
+                for n in range(2):
+                    score_pass(i, n, 1, j0, j1, False, n == 1 and j1 % Q == 0)
+                if j1 % Q == 0:
+                    larger_score(i, j0 // Q)
+        for q in (2, 3):
+            for i in range(4):
+                for n in range(2):
+                    for a in range(2):
+                        apart = q == 3
+                        score_pass(i, n, a, Q * q, Q * (q + 1),
+                                   a == 0 and (apart or n == 0), a == 1 and (apart or n == 1))
                 larger_score(i, q)

from contextlib import ExitStack

import concourse.mybir as mybir
from concourse.masks import make_identity

F32 = mybir.dt.float32
BF16 = mybir.dt.bfloat16
I32 = mybir.dt.int32
U32 = mybir.dt.uint32
U16 = mybir.dt.uint16
U8 = mybir.dt.uint8
FP8X4 = mybir.dt.float8_e4m3fn_x4
FP4X4 = mybir.dt.float4_e2m1fn_x4
ACT = mybir.ActivationFunctionType
ALU = mybir.AluOpType

FLOPS = 3758096384

P = 128
S = 512
T2 = 1024
TA = 2048
TB = 1024
Q = 256
PIECES = ((0, 128), (128, 256), (256, 512), (512, 768), (768, 1024))


def tile_list_wavefront_mode_scores_kernel(
    tc, tab_words, tab_scales, tab2_words, tab2_scales, offs, offs2, offs3, offs4, w1, gain1,
    w2_words, w2_scales, wg1, wg2, refm, wa_words, wa_scales, wb, out,
):
    nc = tc.nc
    with ExitStack() as ctx:
        lists = ctx.enter_context(tc.tile_pool(name="lists", bufs=1))
        keep = ctx.enter_context(tc.tile_pool(name="keep", bufs=1))
        shared = ctx.enter_context(tc.tile_pool(name="shared", bufs=1))
        psum = ctx.enter_context(tc.psum_pool(name="psum", bufs=1))

        def sb(name, shape, dtype, tag=None):
            return keep.tile(shape, dtype, name=name, tag=tag or name, align_bytes=64)

        list1 = lists.tile([P, S // 16], U16, name="list1")
        list2 = lists.tile([P, S // 16], U16, name="list2")
        list3 = lists.tile([P, S // 16], U16, name="list3")
        list4 = lists.tile([P, S // 16], U16, name="list4")
        bank = [psum.tile([P, 512], F32, name="bank%d" % i) for i in range(8)]

        ident = sb("ident", [P, P], F32)
        tabw = [sb("tabw%d" % g, [P, TA], U32, tag="big%d" % g) for g in range(2)]
        tabs = shared.tile([P, TA], U8, name="tabs", offset=0, align_bytes=64)
        tab2w = sb("tab2w", [P, TB], U32)
        tab2s = sb("tab2s", [P, TB], U8)
        vw = [sb("vw%d" % g, [P, S], U32) for g in range(2)]
        vs = sb("vs", [P, S], U8)
        v2w = sb("v2w", [P, S], U32)
        v2s = sb("v2s", [P, S], U8)
        w2w = sb("w2w", [P, 1024], U32)
        w2s = sb("w2s", [P, 1024], U8)
        w2w_dealt = sb("w2w_dealt", [P, 512], U32)
        w2s_dealt = sb("w2s_dealt", [P, 512], U8)
        raw = [shared.tile([P, 2048], F32, name="raw0", offset=20 * T2, align_bytes=64)]
        raw += [sb("raw%d" % i, [P, 2048], F32) for i in range(1, 4)]
        grouped = [
            shared.tile([P, 2048], BF16, name="grouped%d" % i, offset=(40 + 4 * i) * T2, align_bytes=64)
            for i in range(2)
        ]
        grouped += [sb("grouped%d" % i, [P, 2048], BF16) for i in range(2, 6)]
        w1c = [sb("w1c%d" % i, [P, 512], U32) for i in range(4)]
        w1s = [sb("w1s%d" % i, [P, 512], U8) for i in range(4)]
        wbs = [sb("wbs%d" % i, [P, 512], U8) for i in range(2)]
        waw = sb("waw", [P, 2048], U8)
        was = sb("was", [P, 1024], U8)
        wg1n = sb("wg1n", [P, S], F32)
        wg2n = sb("wg2n", [P, S], F32)
        gain = [sb("gain%d" % a, [P, 4], F32) for a in range(2)]
        slope4 = [sb("slope4_%d" % a, [P, 4 * S], F32) for a in range(2)]
        wind4 = [sb("wind4_%d" % a, [P, 4 * S], F32) for a in range(2)]
        th = [slope4[s // 4][:, S * (s % 4) : S * (s % 4 + 1)] for s in range(8)]
        hw = [wind4[s // 4][:, S * (s % 4) : S * (s % 4 + 1)] for s in range(8)]
        for s in range(2):
            th[4 + s] = shared.tile([P, S], F32, name="th%d" % (4 + s), offset=36 * T2 + 4 * S * s, align_bytes=64)[:]
            hw[s] = shared.tile([P, S], F32, name="hw%d" % s, offset=(7 + 8 * s) * T2, align_bytes=64)[:]
        gained4 = sb("gained4", [P, 4 * S], F32)
        ref = [sb("ref%d" % i, [P, T2], F32) for i in range(3)]
        ref.append(shared.tile([P, T2], F32, name="ref3", offset=48 * T2, align_bytes=64))
        page_a = []
        page_b = [sb("page_b%d" % i, [P, T2], F32) for i in range(2)]
        zb = [sb("zb%d" % a, [P, 4 * T2], BF16) for a in range(2)]
        zc = [sb("zc0", [P, 512], U32), None, sb("zc2", [P, 512], U32), sb("zc3", [P, 512], U32)]
        zs = [sb("zs%d" % a, [P, T2], U8) for a in range(2)]

        for plane in (tab2s, w2s, was):
            nc.vector.memset(plane[:].bitcast(I32), 0)
        for page in page_b:
            nc.vector.memset(page[:], 0.0)

        nc.gpsimd.memset(tabs[:].bitcast(I32), 0)

        def load_words(dst, words):
            nc.sync.dma_start(out=dst[:].bitcast(I32), in_=words.rearrange("p t i -> p (t i)").bitcast(I32))

        def load_rows(dst, weight, g, a):
            rows = weight[512 * g : 512 * (g + 1), 512 * a : 512 * (a + 1)]
            nc.sync.dma_start(
                out=dst[:].rearrange("p (j c) -> p j c", j=4), in_=rows.rearrange("(p j) c -> p j c", j=4)
            )

        def load_ref(s):
            if s < 4:
                rows = refm[P * s : P * (s + 1), :]
            else:
                rows = refm[512:1024, :].rearrange("(p t) j -> t p j", t=4)[s - 4]
            nc.sync.dma_start(out=ref[s % 4][:], in_=rows)

        def load_dealt(dst, wg):
            for q in range(4):
                nc.gpsimd.dma_start(out=dst[32 * q : 32 * (q + 1), :], in_=wg.rearrange("(p t) j -> p (t j)", t=4))

        nc.sync.dma_start(list2[:], offs2)
        load_words(tab2w, tab2_words[0])
        for q in range(4):
            nc.sync.dma_start(
                out=tab2s[32 * q : 32 * q + 4, :].bitcast(I32), in_=tab2_scales[0, 4 * q : 4 * q + 4, :].bitcast(I32)
            )
        load_words(w2w, w2_words[0])
        for q in range(4):
            nc.sync.dma_start(
                out=w2s[32 * q : 32 * q + 4, :].bitcast(I32), in_=w2_scales[0, 4 * q : 4 * q + 4, :].bitcast(I32)
            )
        for q in range(4):
            (nc.gpsimd if q < 2 else nc.sync).dma_start(
                out=tabs[32 * q : 32 * q + 8, :].bitcast(I32), in_=tab_scales[:, 4 * q : 4 * q + 4, :].bitcast(I32)
            )
        nc.sync.dma_start(list1[:], offs)
        nc.sync.dma_start(out=wg2n[:], in_=wg2)
        nc.sync.dma_start(list4[:], offs4)
        load_rows(raw[0], w1, 0, 0)
        load_words(tabw[0], tab_words[0])
        load_words(tabw[1], tab_words[1])
        load_rows(raw[1], w1, 1, 0)
        nc.sync.dma_start(out=wg1n[:], in_=wg1)
        with nc.allow_non_contiguous_dma(reason="one gain a partition"):
            nc.sync.dma_start(out=gain[0][:], in_=gain1[0:512].rearrange("(b p) -> p b", p=P))
        nc.sync.dma_start(out=gain[1][:], in_=gain1[512:1024].rearrange("(p t) -> p t", t=4))
        nc.sync.dma_start(list3[:], offs3)
        load_rows(raw[2], w1, 0, 1)
        load_rows(raw[3], w1, 1, 1)
        for s in range(4):
            load_ref(s)

        make_identity(nc, ident[:])

        def cast(values, rows, dealt):
            if dealt:
                dst = values.rearrange("p (t m j) -> p m t j", t=4, j=4)
                src = rows[:].rearrange("p (j m t) -> p m t j", j=4, t=4)
            else:
                dst = values.rearrange("p (c i j) -> p c j i", i=4, j=4)
                src = rows[:].rearrange("p (j c i) -> p c j i", j=4, i=4)
            nc.scalar.copy(out=dst, in_=src)

        def quantize(codes, scales, values):
            nc.vector.quantize_mx(out=codes.bitcast(FP8X4), scales=scales, in_=values)

        def wind_features(s, b):
            cols = slice(P * (s % 4), P * (s % 4 + 1))
            words, scales = (w2w, w2s) if s < 4 else (w2w_dealt, w2s_dealt)
            nc.tensor.matmul_mx(
                out=bank[b][:], lhsT=words[:, cols].bitcast(FP8X4), lhsT_scale=scales[:, cols],
                rhs=v2w[:].bitcast(FP8X4), rhs_scale=v2s[:], start=True, stop=True,
            )
            nc.scalar.copy(out=wind_source(s), in_=bank[b][:])

        def slope_tanh(s, b):
            cols = slice(P * (s % 4), P * (s % 4 + 1))
            for g in (1, 0):
                i = 2 * (s // 4) + g
                nc.tensor.matmul_mx(
                    out=bank[b][:], lhsT=w1c[i][:, cols].bitcast(FP8X4), lhsT_scale=w1s[i][:, cols],
                    rhs=vw[g][:].bitcast(FP8X4), rhs_scale=vs[4 * g : P, :], start=(g == 1), stop=(g == 0),
                )
            nc.scalar.activation(out=th[s], in_=bank[b][:], func=ACT.Tanh)

        def slope_weight(s):
            return (gained4, raw[1])[s // 4][:, S * (s % 4) : S * (s % 4 + 1)]

        def wind_source(s):
            return raw[1][:, 0:S] if s == 3 else hw[s]

        def slope_gain(s):
            nc.scalar.activation(
                out=slope_weight(s) if s < 4 else th[s], in_=wg1n[:] if s < 4 else th[s], func=ACT.Copy,
                scale=gain[s // 4][:, s % 4 : s % 4 + 1]
            )

        def slope_page(s):
            return page_a[s % 4]

        def scatter_a(s):
            nc.vector.tensor_tensor(slope_page(s)[:].indirect(list3[:]), th[s], slope_weight(s), ALU.mult)

        def wind_page(s):
            return page_b[s % 3]

        def scatter_b(s):
            wg = wg2n[:] if s < 4 else wg2_dealt[:, S * (s % 4) : S * (s % 4 + 1)]
            nc.vector.tensor_tensor(wind_page(s)[:].indirect(list4[:]), wind_source(s), wg, ALU.mult)

        def turn(dst, src, start, stop):
            nc.tensor.matmul(dst, src, ident[:], start=start, stop=stop, is_transpose=True)

        def turn_square(s, terms, banks, dst):
            for h in range(2):
                b = bank[banks[h]]
                for n, term in enumerate(terms):
                    for c in range(4):
                        j0 = 512 * h + P * c
                        turn(b[:, P * c : P * (c + 1)], term[:, j0 : j0 + P],
                             n == 0 and c == 0, n == len(terms) - 1 and c == 3)
                if s < 4:
                    nc.scalar.activation(
                        out=dst[h][:, :, :, 32 * s : 32 * (s + 1)],
                        in_=b[:].rearrange("p (c q t) -> p c t q", c=4, t=4), func=ACT.Square,
                    )
                else:
                    j0 = T2 * (s - 4) + 512 * h
                    nc.scalar.activation(out=dst[:, j0 : j0 + 512], in_=b[:], func=ACT.Square)

        def magnitude_turned(jc):
            b = bank[(4, 5, 6, 7, 0, 2, 3, 1)[jc]]
            for n, term in enumerate((qt, st)):
                for t in range(4):
                    turn(b[:, P * t : P * (t + 1)], term[jc // 4][:, jc % 4, t, :],
                         n == 0 and t == 0, n == 1 and t == 3)
            nc.scalar.activation(
                out=zb[0][:, 512 * jc : 512 * (jc + 1)].rearrange("p (j t) -> p j t", t=4),
                in_=b[:].rearrange("p (t j) -> p j t", t=4), func=ACT.Sqrt,
            )

        def magnitude_pair(q):
            b = bank[(0, 2, 3, 1)[q]]
            for n, term in enumerate((slope4[0], gained4)):
                for t in range(2):
                    for c in range(2):
                        j0 = T2 * t + Q * q + P * c
                        turn(b[:, Q * t + P * c : Q * t + P * (c + 1)], term[:, j0 : j0 + P],
                             n == 0 and t == 0 and c == 0, n == 1 and t == 1 and c == 1)
            nc.scalar.activation(
                out=zb[1][:].rearrange("p (j t) -> p j t", t=4)[:, Q * q : Q * (q + 1), 0:2],
                in_=b[:].rearrange("p (t j) -> p j t", t=2), func=ACT.Sqrt,
            )

        def zsq(s):
            return raw[2][:, T2 * (s - 6) : T2 * (s - 5)]

        def add_reference(s):
            nc.vector.tensor_tensor(ref[s % 4][:], slope_page(s)[:], ref[s % 4][:], ALU.add)

        def square_a(s):
            nc.scalar.activation(out=zsq(s), in_=ref[s % 4][:], func=ACT.Square)

        def square_b(s):
            nc.scalar.activation(out=ref[s % 4][:], in_=wind_page(s)[:], func=ACT.Square)

        def add_squares(s, j0, j1):
            nc.vector.tensor_tensor(zsq(s)[:, j0:j1], ref[s % 4][:, j0:j1], zsq(s)[:, j0:j1], ALU.add)

        def root_pair(u, j0, j1):
            nc.scalar.activation(
                out=zb[1][:].rearrange("p (j t) -> p j t", t=4)[:, j0:j1, 2 * u : 2 * u + 2],
                in_=raw[2][:].rearrange("p (t j) -> p j t", t=2)[:, j0:j1, :], func=ACT.Sqrt,
            )

        def z_codes(a, j0, j1):
            h = j0 // 512
            return zc[2 * a + h][:, j0 - 512 * h : j1 - 512 * h]

        def quantize_z(a, j0, j1):
            quantize(z_codes(a, j0, j1), zs[a][:, j0:j1], zb[a][:, 4 * j0 : 4 * j1])

        def score_sum(i, n, q):
            b = bank[i if q == 3 and n == 0 else 4 * (q % 2) + i]
            return b[:, Q * n : Q * (n + 1)]

        def score_pass(i, n, a, j0, j1, start, stop):
            q = j0 // Q
            cols = slice(P * i, P * (i + 1))
            if n == 0:
                codes = waw[:, 1024 * a + 256 * i : 1024 * a + 256 * (i + 1)].bitcast(FP4X4)
                scales = was[:, 512 * a + P * i : 512 * a + P * (i + 1)]
            else:
                codes, scales = wbc[a][:, cols].bitcast(FP8X4), wbs[a][:, cols]
            nc.tensor.matmul_mx(
                out=score_sum(i, n, q)[:, j0 - Q * q : j1 - Q * q], lhsT=codes, lhsT_scale=scales,
                rhs=z_codes(a, j0, j1).bitcast(FP8X4), rhs_scale=zs[a][:, j0:j1], start=start, stop=stop,
            )

        def larger_score(i, q):
            first = slope4[0][:, Q * (4 * (q % 2) + i) : Q * (4 * (q % 2) + i + 1)]
            result = wind4[q // 2][:, S * i + Q * (q % 2) : S * i + Q * (q % 2 + 1)]
            nc.scalar.copy(out=first, in_=score_sum(i, 0, q))
            nc.vector.tensor_tensor(result, score_sum(i, 1, q), first, ALU.max)
            nc.sync.dma_start(out=out[P * i : P * (i + 1), Q * q : Q * (q + 1)], in_=result)

        def slope_square(s):
            banks = ((1, 4), (6, 7), (0, 2), (3, 1), (4, 5), (6, 7))[s]
            turn_square(s, (ref[s % 4], slope_page(s)), banks, st if s < 4 else gained4)
            if s < 4:
                load_ref(s + 4)

        def wind_square(s):
            turn_square(s, (wind_page(s),), ((0, 1), (2, 1), (0, 5), (2, 3), (0, 2), (3, 1))[s], qt if s < 4 else slope4[0])

        nc.vector.tensor_copy(v2w[:], tab2w[:].indirect(list2[:]))
        nc.vector.tensor_copy(v2s[:], tab2s[:].indirect(list2[:]))
        nc.vector.tensor_copy(
            w2w_dealt[:].bitcast(I32).rearrange("p (t m) -> p t m", t=4),
            w2w[:, 512:1024].bitcast(I32).rearrange("p (m t) -> p t m", t=4),
        )
        nc.vector.tensor_copy(
            w2s_dealt[:].rearrange("p (t m) -> p t m", t=4), w2s[:, 512:1024].rearrange("p (m t) -> p t m", t=4)
        )
        nc.vector.tensor_copy(vs[:], tabs[:].indirect(list1[:]))
        page_b.append(shared.tile([P, T2], F32, name="page_b2", offset=0, align_bytes=64))
        nc.gpsimd.memset(page_b[2][:], 0.0)
        for s in range(3):
            wind_features(s, 4 + s)
            scatter_b(s)
        for i in range(4):
            page_a.append(shared.tile([P, T2], F32, name="page_a%d" % i, offset=4 * T2 * (i + 1), align_bytes=64))
            nc.gpsimd.memset(page_a[i][:], 0.0)
        for s in range(4, 7):
            wind_features(s, (2, 3, 7)[s - 4])
        for g in range(2):
            nc.vector.tensor_copy(vw[g][:], tabw[g][:].indirect(list1[:]))
        for i in range(2):
            cast(grouped[i][:], raw[i], False)
            quantize(w1c[i][:], w1s[i][:], grouped[i][:])
        qt_whole = shared.tile([P, 4096], F32, name="qt_whole", offset=20 * T2, align_bytes=64)
        qt = [qt_whole[:, 2048 * h : 2048 * (h + 1)].rearrange("p (c t r) -> p c t r", c=4, t=4) for h in range(2)]
        wind_square(0)
        wind_square(1)
        wind_features(3, 1)
        scatter_b(3)
        wg2_dealt = shared.tile([P, 4 * S], F32, name="wg2_dealt", offset=40 * T2, align_bytes=64)
        load_dealt(wg2_dealt, wg2)
        load_dealt(raw[1], wg1)
        st_flat = [sb("st%d" % h, [P, 4 * S], F32, tag="big%d" % h) for h in range(2)]
        st = [half[:].rearrange("p (c t r) -> p c t r", c=4, t=4) for half in st_flat]
        for s in range(4):
            slope_gain(s)
        for s in range(4):
            slope_tanh(s, (0, 5, 6, 7)[s])
            scatter_a(s)
        for i in (2, 3):
            cast(grouped[i][:], raw[i], True)
            quantize(w1c[i][:], w1s[i][:], grouped[i][:])
            load_rows(raw[i], wb, i - 2, 0)
        for q in range(4):
            nc.sync.dma_start(
                out=was[32 * q : 32 * q + 4, :].bitcast(I32).rearrange("p (a n) -> p a n", a=2),
                in_=wa_scales[:, 4 * q : 4 * q + 4, :].bitcast(I32).rearrange("a r n -> r a n"),
            )
        nc.sync.dma_start(
            out=waw[:].bitcast(I32).rearrange("p (a c) -> p a c", a=2),
            in_=wa_words.bitcast(I32).rearrange("a p c -> p a c"),
        )
        wind_square(2)
        wind_square(3)
        for s in range(4):
            if s >= 2:
                cast(grouped[s + 2][:], raw[s], False)
            slope_square(s)
        for s in range(4, 8):
            slope_tanh(s, (0, 2, 3, 1)[s - 4])
            slope_gain(s)
        for s in range(4, 7):
            scatter_b(s)
        for s in (4, 6, 5):
            scatter_a(s)
        add_reference(6)
        scatter_a(7)
        wind_square(4)
        wind_square(5)
        for jc in range(8):
            magnitude_turned(jc)
        slope_square(4)
        slope_square(5)
        square_a(6)
        square_b(6)
        add_reference(7)
        wbc = [shared.tile([P, 512], U32, name="wbc0", offset=36 * T2, align_bytes=64)]
        quantize(wbc[0][:], wbs[0][:], grouped[4][:])
        quantize_z(0, 0, 512)
        add_squares(6, 0, T2)
        hw[7] = shared.tile([P, S], F32, name="hw7", offset=16 * T2, align_bytes=64)[:]
        wind_features(7, 6)
        scatter_b(7)
        square_a(7)
        for q in range(4):
            magnitude_pair(q)
        for q in range(2):
            for i in range(4):
                for n in range(2):
                    score_pass(i, n, 0, Q * q, Q * (q + 1), n == 0, False)
        last = wind_page(7)
        first_square = shared.tile([P, Q], F32, name="first_square", offset=38 * T2, align_bytes=64)
        for j0, j1 in PIECES[:2]:
            nc.vector.tensor_tensor(first_square[:, j0:j1], last[:, j0:j1], last[:, j0:j1], ALU.mult)
        nc.scalar.activation(out=ref[3][:, Q:T2], in_=last[:, Q:T2], func=ACT.Square)
        for j0, j1 in PIECES:
            square = first_square[:, j0:j1] if j0 < Q else ref[3][:, j0:j1]
            nc.vector.tensor_tensor(zsq(7)[:, j0:j1], square, zsq(7)[:, j0:j1], ALU.add)
            root_pair(1, j0, j1)
            quantize_z(1, j0, j1)
        wbc.append(shared.tile([P, 512], U32, name="wbc1", offset=38 * T2, align_bytes=64))
        quantize(wbc[1][:], wbs[1][:], grouped[5][:])
        zc[1] = shared.tile([P, 512], U32, name="zc1", offset=48 * T2, align_bytes=64)
        quantize_z(0, 512, T2)
        for j0, j1 in PIECES[:3]:
            for i in range(4):
                for n in range(2):
                    score_pass(i, n, 1, j0, j1, False, n == 1 and j1 % Q == 0)
                if j1 % Q == 0:
                    larger_score(i, j0 // Q)
        for q in (2, 3):
            for i in range(4):
                for n in range(2):
                    for a in range(2):
                        apart = q == 3
                        score_pass(i, n, a, Q * q, Q * (q + 1),
                                   a == 0 and (apart or n == 0), a == 1 and (apart or n == 1))
                larger_score(i, q)
